import numpy as np
import ml_dtypes


def mxq(x, axis, fmt="e4m3"):
    dtype, down = {"e4m3": (ml_dtypes.float8_e4m3fn, 7), "e5m2": (ml_dtypes.float8_e5m2, 14)}[fmt]
    v = np.moveaxis(np.asarray(x, np.float32).astype(ml_dtypes.bfloat16).astype(np.float64), axis, -1)
    blocks = v.reshape(v.shape[:-1] + (-1, 32))
    amax = np.abs(blocks).max(-1, keepdims=True)
    byte = np.maximum(np.where(amax > 0, np.frexp(amax)[1] - 1 + 127, 0) - down, 1)
    scale = np.exp2(byte - 127.0)
    codes = (blocks / scale).astype(np.float32).astype(dtype).astype(np.float64)
    return np.moveaxis((codes * scale).reshape(v.shape), -1, axis)


WIDE = False


def mx_kscale(k):
    if not WIDE:
        return np.ones(k)
    levels = np.array([10, -10, 5, -5, 0])
    if k % 512:
        return np.exp2(np.random.permutation(np.resize(levels, k // 32))).repeat(32)
    a = np.empty((k // 512, 16))
    for p in range(k // 512):
        a[p, :8] = np.random.permutation(np.resize(levels, 8))
        for g in range(8):
            far = levels[np.abs(levels - a[p, g]) >= 10]
            a[p, g + 8] = far[np.random.randint(len(far))]
    return np.exp2(a.ravel()).repeat(32)


def f64(x):
    return np.asarray(x).astype(np.float64)


def striped(idx):
    return np.tile(idx.reshape(-1, 16).T, (8, 1)).astype(np.uint16)


def unstriped(offs):
    return offs[:16].T.reshape(-1).astype(np.int64)


def pack_weight(w):
    k, n = w.shape
    w = f64(np.asarray(w, np.float32).astype(ml_dtypes.bfloat16)).reshape(k // 32, 32, n)
    amax = np.abs(w).max(1)
    byte = np.clip(np.where(amax > 0, np.frexp(amax)[1] - 1 + 127 - 7, 1), 1, 254)
    scaled = (w * np.exp2(127.0 - byte)[:, None, :]).reshape(k, n).astype(np.float32)
    words = np.ascontiguousarray(scaled.reshape(k // 512, 128, 4, n).transpose(0, 1, 3, 2)).astype(ml_dtypes.float8_e4m3fn).view(np.uint8)
    return words, np.ascontiguousarray(byte.astype(np.uint8).reshape(k // 512, 16, n))


def unpack_weight(words, scales):
    g, p, n, _ = words.shape
    vals = np.ascontiguousarray(words).view(ml_dtypes.float8_e4m3fn).astype(np.float64) * np.repeat(np.exp2(scales.astype(np.float64) - 127.0), 8, axis=1)[..., None]
    return vals.transpose(0, 1, 3, 2).reshape(g * 512, n)


def relu(v):
    return np.maximum(v, 0.0)


K, T, S, H, N = 512, 1024, 512, 512, 256


def setup_inputs():
    n = np.random.standard_normal
    s = mx_kscale(K)[:, None]
    u = mx_kscale(H)
    packed_xT = pack_weight(n((K, T)) * s)
    packed_w2 = pack_weight(n((H, N)) / np.sqrt(H) / u[:, None])
    return {
        "x_words": packed_xT[0],
        "x_scales": packed_xT[1],
        "w1": (n((K, H)) / np.sqrt(K) / s * u).astype(np.float32),
        "w2_words": packed_w2[0],
        "w2_scales": packed_w2[1],
        "offs": striped(np.random.permutation(T)[:S]),
    }


def reference(x_words, x_scales, w1, w2_words, w2_scales, offs):
    xq = unpack_weight(x_words, x_scales)[:, unstriped(offs)]
    h = relu(mxq(f64(w1), 0, "e4m3").T @ xq)
    z = h - h.mean(axis=1, keepdims=True)
    return unpack_weight(w2_words, w2_scales).T @ mxq(z, 0, "e4m3")

@@ -1,0 +1,126 @@
+from contextlib import ExitStack
+
+import concourse.mybir as mybir
+
+K, T, S, H, N = 512, 1024, 512, 512, 256
+FLOPS = 2 * K * H * S + 2 * H * N * S
+
+F32 = mybir.dt.float32
+BF16 = mybir.dt.bfloat16
+I32 = mybir.dt.int32
+U32 = mybir.dt.uint32
+U16 = mybir.dt.uint16
+U8 = mybir.dt.uint8
+FP8X4 = mybir.dt.float8_e4m3fn_x4
+ACT = mybir.ActivationFunctionType
+ALU = mybir.AluOpType
+
+P = 128
+PACK = 4
+HALF = 256
+CHUNK = 128
+
+
+def tile_picked_deepset_relu_p_kernel(tc, x_words, x_scales, w1, w2_words, w2_scales, offs, out):
+    nc = tc.nc
+    with ExitStack() as ctx:
+        keep = ctx.enter_context(tc.tile_pool(name="keep", bufs=1))
+        reuse = ctx.enter_context(tc.tile_pool(name="reuse", bufs=1))
+        psum = ctx.enter_context(tc.psum_pool(name="psum", bufs=1))
+
+        offsets = keep.tile([P, S // 16], U16, name="offsets")
+        xw = keep.tile([P, T], U32, name="xw", align_bytes=64)
+        xs = reuse.tile([P, T], U8, name="xs", align_bytes=64, offset=1536)
+        w2s = keep.tile([P, N], U8, name="w2s", align_bytes=64)
+        raw = [keep.tile([P, PACK, HALF], F32, name="raw%d" % a, tag="raw%d" % a, align_bytes=64) for a in range(2)]
+
+        nc.vector.memset(xs[:].bitcast(I32), 0)
+        nc.vector.memset(w2s[:].bitcast(I32), 0)
+
+        w1_rows = w1.rearrange("(p j) c -> p j c", j=PACK)
+        nc.sync.dma_start(offsets[:], offs)
+        for q in range(4):
+            nc.sync.dma_start(xs[32 * q : 32 * q + 4, :].bitcast(I32), x_scales[0, 4 * q : 4 * q + 4, :].bitcast(I32))
+        nc.scalar.dma_start(raw[0][:], w1_rows[:, :, 0:HALF])
+        nc.scalar.dma_start(xw[:].bitcast(I32), x_words[0].rearrange("p n t -> p (n t)").bitcast(I32))
+        nc.scalar.dma_start(raw[1][:], w1_rows[:, :, HALF : 2 * HALF])
+        for q in range(4):
+            nc.sync.dma_start(w2s[32 * q : 32 * q + 4, :].bitcast(I32), w2_scales[0, 4 * q : 4 * q + 4, :].bitcast(I32))
+
+        table_warm = keep.tile([P, 2], F32, name="table_warm")
+        nc.gpsimd.memset(table_warm[:, 0:1], 0.0)
+        nc.scalar.activation(table_warm[:, 1:2], table_warm[:, 0:1], ACT.Relu)
+
+        xgs = keep.tile([P, S], U8, name="xgs", align_bytes=64)
+        xg = reuse.tile([P, S], U32, name="xg", align_bytes=64, offset=0)
+        nc.vector.tensor_copy(xgs[:], xs[:].indirect(offsets[:]))
+
+        MH = HALF // PACK
+        grouped = reuse.tile([P, PACK, P, PACK], BF16, name="grouped", align_bytes=64, offset=2048)
+        wq = [keep.tile([P, P], U32, name="wq%d" % t, align_bytes=64) for t in range(PACK)]
+        ws = [keep.tile([P, P], U8, name="ws%d" % t, align_bytes=64) for t in range(PACK)]
+
+        def cast(copy, a, m0, m1):
+            dst = grouped[:, :, a * MH + m0 : a * MH + m1, :].rearrange("p t m j -> p m j t")
+            src = raw[a][:, :, PACK * m0 : PACK * m1].rearrange("p j (m t) -> p m j t", t=PACK)
+            copy(dst, src)
+
+        cast(nc.scalar.copy, 0, 0, MH)
+        w2w = keep.tile([P, N], U32, name="w2w", tag="raw0", align_bytes=64)
+        nc.sync.dma_start(w2w[:].bitcast(I32), w2_words[0].rearrange("p n t -> p (n t)").bitcast(I32))
+        nc.vector.tensor_copy(xg[:], xw[:].indirect(offsets[:]))
+        cast(nc.scalar.copy, 1, 0, 24)
+        cast(nc.vector.tensor_copy, 1, 24, MH)
+
+        h = [keep.tile([P, S], F32, name="h%d" % t, align_bytes=64) for t in range(PACK)]
+        mean = [keep.tile([P, 1], F32, name="mean%d" % t) for t in range(PACK)]
+        pairs = [keep.tile([P, 2, 2 * HALF], BF16, name="pairs%d" % b, align_bytes=64) for b in range(2)]
+        for t in range(PACK):
+            nc.vector.quantize_mx(
+                out=wq[t][:].bitcast(FP8X4),
+                scales=ws[t][:],
+                in_=grouped[:, t, :, :].rearrange("p m j -> p (m j)"),
+            )
+        for t in range(PACK):
+            acc = psum.tile([P, S], F32, name="acc%d" % t, tag="acc%d" % t)
+            nc.tensor.matmul_mx(
+                out=acc[:], lhsT=wq[t][:].bitcast(FP8X4), lhsT_scale=ws[t][:],
+                rhs=xg[:].bitcast(FP8X4), rhs_scale=xgs[:], start=True, stop=True,
+            )
+            nc.scalar.activation(h[t][:], acc[:], ACT.Relu, scale=1.0 / S, accum_out=mean[t][:])
+            for b in range(2):
+                nc.vector.tensor_scalar(
+                    out=pairs[b][:, t // 2, t % 2 : 2 * HALF : 2], in0=h[t][:, b * HALF : (b + 1) * HALF],
+                    scalar1=float(S), scalar2=mean[t][:], op0=ALU.mult, op1=ALU.subtract,
+                )
+
+        chunks = S // CHUNK
+        zi = [keep.tile([P, PACK * CHUNK], BF16, name="zi%d" % c, align_bytes=64) for c in range(chunks)]
+        zq = [keep.tile([P, CHUNK], U32, name="zq%d" % c, align_bytes=64) for c in range(chunks)]
+        zs = [keep.tile([P, CHUNK], U8, name="zs%d" % c, align_bytes=64) for c in range(chunks)]
+        for c in range(chunks):
+            b, i = divmod(c, 2)
+            dst = zi[c][:].bitcast(F32).rearrange("p (n u) -> p n u", u=2)
+            src = pairs[b][:].bitcast(F32)[:, :, i * CHUNK : (i + 1) * CHUNK].rearrange("p u n -> p n u")
+            if b == 0:
+                nc.vector.tensor_copy(dst, src)
+            else:
+                nc.scalar.copy(dst, src)
+        for c in range(chunks):
+            nc.vector.quantize_mx(out=zq[c][:].bitcast(FP8X4), scales=zs[c][:], in_=zi[c][:])
+
+        out_rows = out.rearrange("(m p) n -> p m n", p=P)
+        for c in range(chunks):
+            res = psum.tile([P, 2, CHUNK], F32, name="res%d" % c, tag="res%d" % c)
+            for m in range(2):
+                rows = slice(m * P, (m + 1) * P)
+                nc.tensor.matmul_mx(
+                    out=res[:, m, :], lhsT=w2w[:, rows].bitcast(FP8X4), lhsT_scale=w2s[:, rows],
+                    rhs=zq[c][:].bitcast(FP8X4), rhs_scale=zs[c][:], start=True, stop=True,
+                )
+            o = keep.tile([P, 2, CHUNK], F32, name="o%d" % c)
+            if c % 2 == 0:
+                nc.scalar.copy(o[:], res[:])
+            else:
+                nc.vector.tensor_copy(o[:], res[:])
+            nc.sync.dma_start(out_rows[:, :, c * CHUNK : (c + 1) * CHUNK], o[:])

@@ -25,38 +25,34 @@ def tile_picked_deepset_relu_p_kernel(tc, x_words, x_scales, w1, w2_words, w2_sc
     nc = tc.nc
     with ExitStack() as ctx:
         keep = ctx.enter_context(tc.tile_pool(name="keep", bufs=1))
-        reuse = ctx.enter_context(tc.tile_pool(name="reuse", bufs=1))
         psum = ctx.enter_context(tc.psum_pool(name="psum", bufs=1))
 
         offsets = keep.tile([P, S // 16], U16, name="offsets")
         xw = keep.tile([P, T], U32, name="xw", align_bytes=64)
-        xs = reuse.tile([P, T], U8, name="xs", align_bytes=64, offset=1536)
-        w2s = keep.tile([P, N], U8, name="w2s", align_bytes=64)
+        xs = keep.tile([P, T], U8, name="xs", tag="scales", align_bytes=64)
         raw = [keep.tile([P, PACK, HALF], F32, name="raw%d" % a, tag="raw%d" % a, align_bytes=64) for a in range(2)]
 
         nc.vector.memset(xs[:].bitcast(I32), 0)
-        nc.vector.memset(w2s[:].bitcast(I32), 0)
 
         w1_rows = w1.rearrange("(p j) c -> p j c", j=PACK)
         nc.sync.dma_start(offsets[:], offs)
         for q in range(4):
             nc.sync.dma_start(xs[32 * q : 32 * q + 4, :].bitcast(I32), x_scales[0, 4 * q : 4 * q + 4, :].bitcast(I32))
-        nc.scalar.dma_start(raw[0][:], w1_rows[:, :, 0:HALF])
         nc.scalar.dma_start(xw[:].bitcast(I32), x_words[0].rearrange("p n t -> p (n t)").bitcast(I32))
-        nc.scalar.dma_start(raw[1][:], w1_rows[:, :, HALF : 2 * HALF])
+        nc.sync.dma_start(raw[0][:], w1_rows[:, :, 0:HALF])
+        nc.sync.dma_start(raw[1][:], w1_rows[:, :, HALF : 2 * HALF])
+
+        xgs = keep.tile([P, S], U8, name="xgs", align_bytes=64)
+        xg = keep.tile([P, S], U32, name="xg", align_bytes=64)
+        nc.vector.tensor_copy(xg[:], xw[:].indirect(offsets[:]))
+        nc.vector.tensor_copy(xgs[:], xs[:].indirect(offsets[:]))
+        w2s = keep.tile([P, N], U8, name="w2s", tag="scales", align_bytes=64)
+        nc.gpsimd.memset(w2s[:].bitcast(I32), 0)
         for q in range(4):
             nc.sync.dma_start(w2s[32 * q : 32 * q + 4, :].bitcast(I32), w2_scales[0, 4 * q : 4 * q + 4, :].bitcast(I32))
 
-        table_warm = keep.tile([P, 2], F32, name="table_warm")
-        nc.gpsimd.memset(table_warm[:, 0:1], 0.0)
-        nc.scalar.activation(table_warm[:, 1:2], table_warm[:, 0:1], ACT.Relu)
-
-        xgs = keep.tile([P, S], U8, name="xgs", align_bytes=64)
-        xg = reuse.tile([P, S], U32, name="xg", align_bytes=64, offset=0)
-        nc.vector.tensor_copy(xgs[:], xs[:].indirect(offsets[:]))
-
         MH = HALF // PACK
-        grouped = reuse.tile([P, PACK, P, PACK], BF16, name="grouped", align_bytes=64, offset=2048)
+        grouped = keep.tile([P, PACK, P, PACK], BF16, name="grouped", align_bytes=64)
         wq = [keep.tile([P, P], U32, name="wq%d" % t, align_bytes=64) for t in range(PACK)]
         ws = [keep.tile([P, P], U8, name="ws%d" % t, align_bytes=64) for t in range(PACK)]
 
@@ -68,7 +64,6 @@ def tile_picked_deepset_relu_p_kernel(tc, x_words, x_scales, w1, w2_words, w2_sc
         cast(nc.scalar.copy, 0, 0, MH)
         w2w = keep.tile([P, N], U32, name="w2w", tag="raw0", align_bytes=64)
         nc.sync.dma_start(w2w[:].bitcast(I32), w2_words[0].rearrange("p n t -> p (n t)").bitcast(I32))
-        nc.vector.tensor_copy(xg[:], xw[:].indirect(offsets[:]))
         cast(nc.scalar.copy, 1, 0, 24)
         cast(nc.vector.tensor_copy, 1, 24, MH)
 

@@ -35,17 +35,25 @@ def tile_picked_deepset_relu_p_kernel(tc, x_words, x_scales, w1, w2_words, w2_sc
         nc.vector.memset(xs[:].bitcast(I32), 0)
 
         w1_rows = w1.rearrange("(p j) c -> p j c", j=PACK)
+        nc.scalar.dma_start(xw[:].bitcast(I32), x_words[0].rearrange("p n t -> p (n t)").bitcast(I32))
         nc.sync.dma_start(offsets[:], offs)
         for q in range(4):
-            nc.sync.dma_start(xs[32 * q : 32 * q + 4, :].bitcast(I32), x_scales[0, 4 * q : 4 * q + 4, :].bitcast(I32))
-        nc.scalar.dma_start(xw[:].bitcast(I32), x_words[0].rearrange("p n t -> p (n t)").bitcast(I32))
+            queue = nc.sync if q < 2 else nc.scalar
+            queue.dma_start(xs[32 * q : 32 * q + 4, :].bitcast(I32), x_scales[0, 4 * q : 4 * q + 4, :].bitcast(I32))
         nc.sync.dma_start(raw[0][:], w1_rows[:, :, 0:HALF])
         nc.sync.dma_start(raw[1][:], w1_rows[:, :, HALF : 2 * HALF])
 
         xgs = keep.tile([P, S], U8, name="xgs", align_bytes=64)
         xg = keep.tile([P, S], U32, name="xg", align_bytes=64)
         nc.vector.tensor_copy(xg[:], xw[:].indirect(offsets[:]))
-        nc.vector.tensor_copy(xgs[:], xs[:].indirect(offsets[:]))
+        nc.vector.tensor_copy(xgs[:, 0:CHUNK], xs[:].indirect(offsets[:, 0 : CHUNK // 16]))
+        nc.vector.tensor_copy(xgs[:, CHUNK:S], xs[:].indirect(offsets[:, CHUNK // 16 : S // 16]))
+        pre = psum.tile([32, PACK, CHUNK], F32, name="pre", tag="res3")
+        for i in range(10):
+            nc.tensor.matmul_mx(
+                out=pre[:, i % PACK, :], lhsT=xg[:, 0:32].bitcast(FP8X4), lhsT_scale=xgs[:, 0:32],
+                rhs=xg[:, 0:CHUNK].bitcast(FP8X4), rhs_scale=xgs[:, 0:CHUNK], start=True, stop=True,
+            )
         w2s = keep.tile([P, N], U8, name="w2s", tag="scales", align_bytes=64)
         nc.gpsimd.memset(w2s[:].bitcast(I32), 0)
         for q in range(4):
@@ -88,6 +96,12 @@ def tile_picked_deepset_relu_p_kernel(tc, x_words, x_scales, w1, w2_words, w2_sc
                     out=pairs[b][:, t // 2, t % 2 : 2 * HALF : 2], in0=h[t][:, b * HALF : (b + 1) * HALF],
                     scalar1=float(S), scalar2=mean[t][:], op0=ALU.mult, op1=ALU.subtract,
                 )
+        for t in range(PACK - 3, PACK):
+            spin = psum.tile([32, S], F32, name="spin%d" % t, tag="acc%d" % t)
+            nc.tensor.matmul_mx(
+                out=spin[:], lhsT=wq[0][:, 0:32].bitcast(FP8X4), lhsT_scale=ws[0][:, 0:32],
+                rhs=xg[:].bitcast(FP8X4), rhs_scale=xgs[:], start=True, stop=True,
+            )
 
         chunks = S // CHUNK
         zi = [keep.tile([P, PACK * CHUNK], BF16, name="zi%d" % c, align_bytes=64) for c in range(chunks)]
@@ -105,14 +119,24 @@ def tile_picked_deepset_relu_p_kernel(tc, x_words, x_scales, w1, w2_words, w2_sc
             nc.vector.quantize_mx(out=zq[c][:].bitcast(FP8X4), scales=zs[c][:], in_=zi[c][:])
 
         out_rows = out.rearrange("(m p) n -> p m n", p=P)
-        for c in range(chunks):
+
+        def second_layer(c, m, res):
+            rows = slice(m * P, (m + 1) * P)
+            nc.tensor.matmul_mx(
+                out=res, lhsT=w2w[:, rows].bitcast(FP8X4), lhsT_scale=w2s[:, rows],
+                rhs=zq[c][:].bitcast(FP8X4), rhs_scale=zs[c][:], start=True, stop=True,
+            )
+
+        for m in range(2):
+            first = psum.tile([P, CHUNK], F32, name="first%d" % m, tag=("res0", "acc0")[m])
+            second_layer(0, m, first[:])
+            o = keep.tile([P, CHUNK], F32, name="ofirst%d" % m)
+            nc.scalar.copy(o[:], first[:])
+            nc.sync.dma_start(out_rows[:, m, 0:CHUNK], o[:])
+        for c in range(1, chunks):
             res = psum.tile([P, 2, CHUNK], F32, name="res%d" % c, tag="res%d" % c)
             for m in range(2):
-                rows = slice(m * P, (m + 1) * P)
-                nc.tensor.matmul_mx(
-                    out=res[:, m, :], lhsT=w2w[:, rows].bitcast(FP8X4), lhsT_scale=w2s[:, rows],
-                    rhs=zq[c][:].bitcast(FP8X4), rhs_scale=zs[c][:], start=True, stop=True,
-                )
+                second_layer(c, m, res[:, m, :])
             o = keep.tile([P, 2, CHUNK], F32, name="o%d" % c)
             if c % 2 == 0:
                 nc.scalar.copy(o[:], res[:])

@@ -72,30 +72,54 @@ def tile_picked_deepset_relu_p_kernel(tc, x_words, x_scales, w1, w2_words, w2_sc
         cast(nc.scalar.copy, 0, 0, MH)
         w2w = keep.tile([P, N], U32, name="w2w", tag="raw0", align_bytes=64)
         nc.sync.dma_start(w2w[:].bitcast(I32), w2_words[0].rearrange("p n t -> p (n t)").bitcast(I32))
-        cast(nc.scalar.copy, 1, 0, 24)
-        cast(nc.vector.tensor_copy, 1, 24, MH)
+        cast(nc.scalar.copy, 1, 0, 26)
+        cast(nc.vector.tensor_copy, 1, 26, MH)
 
         h = [keep.tile([P, S], F32, name="h%d" % t, align_bytes=64) for t in range(PACK)]
         mean = [keep.tile([P, 1], F32, name="mean%d" % t) for t in range(PACK)]
-        pairs = [keep.tile([P, 2, 2 * HALF], BF16, name="pairs%d" % b, align_bytes=64) for b in range(2)]
+        chunks = S // CHUNK
+        zi = [keep.tile([P, PACK * CHUNK], BF16, name="zi%d" % c, align_bytes=64) for c in range(chunks)]
+        pairs_one = keep.tile([P, 2, 2 * CHUNK], BF16, name="pairs_one", align_bytes=64)
+        pairs_high = keep.tile([P, 2, 2 * HALF], BF16, name="pairs_high", align_bytes=64)
         for t in range(PACK):
             nc.vector.quantize_mx(
                 out=wq[t][:].bitcast(FP8X4),
                 scales=ws[t][:],
                 in_=grouped[:, t, :, :].rearrange("p m j -> p (m j)"),
             )
-        for t in range(PACK):
-            acc = psum.tile([P, S], F32, name="acc%d" % t, tag="acc%d" % t)
+        def first_layer(t, cols, acc):
             nc.tensor.matmul_mx(
-                out=acc[:], lhsT=wq[t][:].bitcast(FP8X4), lhsT_scale=ws[t][:],
-                rhs=xg[:].bitcast(FP8X4), rhs_scale=xgs[:], start=True, stop=True,
+                out=acc, lhsT=wq[t][:].bitcast(FP8X4), lhsT_scale=ws[t][:],
+                rhs=xg[:, cols].bitcast(FP8X4), rhs_scale=xgs[:, cols], start=True, stop=True,
             )
+
+        part_mean = keep.tile([P, 1], F32, name="part_mean")
+        part_sum = keep.tile([P, 1], F32, name="part_sum")
+        low = psum.tile([P, HALF], F32, name="low", tag="acc0")
+        high = psum.tile([P, HALF], F32, name="high", tag="res2")
+        first_layer(0, slice(0, HALF), low[:])
+        first_layer(0, slice(HALF, S), high[:])
+        nc.scalar.activation(h[0][:, 0:HALF], low[:], ACT.Relu, scale=1.0 / S, accum_out=part_mean[:])
+        nc.vector.tensor_scalar(
+            out=h[0][:, HALF:S], in0=high[:], scalar1=0.0, scalar2=None, op0=ALU.max, op1=ALU.add, accum_out=part_sum[:]
+        )
+        nc.vector.tensor_scalar(
+            out=mean[0][:], in0=part_sum[:], scalar1=1.0 / S, scalar2=part_mean[:], op0=ALU.mult, op1=ALU.add
+        )
+        for t in range(1, PACK):
+            acc = psum.tile([P, S], F32, name="acc%d" % t, tag="acc%d" % t)
+            first_layer(t, slice(0, S), acc[:])
             nc.scalar.activation(h[t][:], acc[:], ACT.Relu, scale=1.0 / S, accum_out=mean[t][:])
-            for b in range(2):
-                nc.vector.tensor_scalar(
-                    out=pairs[b][:, t // 2, t % 2 : 2 * HALF : 2], in0=h[t][:, b * HALF : (b + 1) * HALF],
-                    scalar1=float(S), scalar2=mean[t][:], op0=ALU.mult, op1=ALU.subtract,
-                )
+        def centre(t, dst, cols):
+            nc.vector.tensor_scalar(
+                out=dst, in0=h[t][:, cols], scalar1=1.0 if t == 0 and cols.start >= HALF else float(S), scalar2=mean[t][:],
+                op0=ALU.mult, op1=ALU.subtract,
+            )
+
+        for t in range(PACK):
+            centre(t, zi[0][:, t : PACK * CHUNK : PACK], slice(0, CHUNK))
+            centre(t, pairs_high[:, t // 2, t % 2 : 2 * HALF : 2], slice(HALF, S))
+            centre(t, pairs_one[:, t // 2, t % 2 : 2 * CHUNK : 2], slice(CHUNK, HALF))
         for t in range(PACK - 3, PACK):
             spin = psum.tile([32, S], F32, name="spin%d" % t, tag="acc%d" % t)
             nc.tensor.matmul_mx(
@@ -103,20 +127,22 @@ def tile_picked_deepset_relu_p_kernel(tc, x_words, x_scales, w1, w2_words, w2_sc
                 rhs=xg[:].bitcast(FP8X4), rhs_scale=xgs[:], start=True, stop=True,
             )
 
-        chunks = S // CHUNK
-        zi = [keep.tile([P, PACK * CHUNK], BF16, name="zi%d" % c, align_bytes=64) for c in range(chunks)]
         zq = [keep.tile([P, CHUNK], U32, name="zq%d" % c, align_bytes=64) for c in range(chunks)]
         zs = [keep.tile([P, CHUNK], U8, name="zs%d" % c, align_bytes=64) for c in range(chunks)]
-        for c in range(chunks):
-            b, i = divmod(c, 2)
+
+        def weave(copy, c, pairs, first):
             dst = zi[c][:].bitcast(F32).rearrange("p (n u) -> p n u", u=2)
-            src = pairs[b][:].bitcast(F32)[:, :, i * CHUNK : (i + 1) * CHUNK].rearrange("p u n -> p n u")
-            if b == 0:
-                nc.vector.tensor_copy(dst, src)
-            else:
-                nc.scalar.copy(dst, src)
-        for c in range(chunks):
+            copy(dst, pairs[:].bitcast(F32)[:, :, first : first + CHUNK].rearrange("p u n -> p n u"))
+
+        def quantize_z(c):
             nc.vector.quantize_mx(out=zq[c][:].bitcast(FP8X4), scales=zs[c][:], in_=zi[c][:])
+
+        weave(nc.scalar.copy, 2, pairs_high, 0)
+        weave(nc.scalar.copy, 3, pairs_high, CHUNK)
+        quantize_z(0)
+        weave(nc.vector.tensor_copy, 1, pairs_one, 0)
+        for c in (2, 1, 3):
+            quantize_z(c)
 
         out_rows = out.rearrange("(m p) n -> p m n", p=P)
 
@@ -127,19 +153,23 @@ def tile_picked_deepset_relu_p_kernel(tc, x_words, x_scales, w1, w2_words, w2_sc
                 rhs=zq[c][:].bitcast(FP8X4), rhs_scale=zs[c][:], start=True, stop=True,
             )
 
-        for m in range(2):
-            first = psum.tile([P, CHUNK], F32, name="first%d" % m, tag=("res0", "acc0")[m])
-            second_layer(0, m, first[:])
-            o = keep.tile([P, CHUNK], F32, name="ofirst%d" % m)
-            nc.scalar.copy(o[:], first[:])
-            nc.sync.dma_start(out_rows[:, m, 0:CHUNK], o[:])
-        for c in range(1, chunks):
+        def finish_whole(c, copy):
             res = psum.tile([P, 2, CHUNK], F32, name="res%d" % c, tag="res%d" % c)
             for m in range(2):
                 second_layer(c, m, res[:, m, :])
             o = keep.tile([P, 2, CHUNK], F32, name="o%d" % c)
-            if c % 2 == 0:
-                nc.scalar.copy(o[:], res[:])
-            else:
-                nc.vector.tensor_copy(o[:], res[:])
+            copy(o[:], res[:])
             nc.sync.dma_start(out_rows[:, :, c * CHUNK : (c + 1) * CHUNK], o[:])
+
+        def finish_split(c, copies, tags):
+            for m in range(2):
+                res = psum.tile([P, CHUNK], F32, name="res%d_%d" % (c, m), tag=tags[m])
+                second_layer(c, m, res[:])
+                o = keep.tile([P, CHUNK], F32, name="o%d_%d" % (c, m))
+                copies[m](o[:], res[:])
+                nc.sync.dma_start(out_rows[:, m, c * CHUNK : (c + 1) * CHUNK], o[:])
+
+        finish_split(0, (nc.scalar.copy, nc.scalar.copy), ("res0", "acc0"))
+        finish_whole(2, nc.scalar.copy)
+        finish_whole(1, nc.vector.tensor_copy)
+        finish_split(3, (nc.scalar.copy, nc.vector.tensor_copy), ("res3", "acc1"))

@@ -29,119 +29,91 @@ def tile_picked_deepset_relu_p_kernel(tc, x_words, x_scales, w1, w2_words, w2_sc
 
         offsets = keep.tile([P, S // 16], U16, name="offsets")
         xw = keep.tile([P, T], U32, name="xw", align_bytes=64)
-        xs = keep.tile([P, T], U8, name="xs", tag="scales", align_bytes=64)
-        raw = [keep.tile([P, PACK, HALF], F32, name="raw%d" % a, tag="raw%d" % a, align_bytes=64) for a in range(2)]
+        xs = keep.tile([P, T], U8, name="xs", align_bytes=64)
+        w2s = keep.tile([P, N], U8, name="w2s", align_bytes=64)
+        raw = [keep.tile([P, 2, H], F32, name="raw%d" % u, tag="raw%d" % u, align_bytes=64) for u in range(2)]
 
         nc.vector.memset(xs[:].bitcast(I32), 0)
+        nc.vector.memset(w2s[:].bitcast(I32), 0)
 
         w1_rows = w1.rearrange("(p j) c -> p j c", j=PACK)
-        nc.scalar.dma_start(xw[:].bitcast(I32), x_words[0].rearrange("p n t -> p (n t)").bitcast(I32))
+        nc.scalar.dma_start(raw[0][:], w1_rows[:, 0:2, :])
         nc.sync.dma_start(offsets[:], offs)
         for q in range(4):
             queue = nc.sync if q < 2 else nc.scalar
             queue.dma_start(xs[32 * q : 32 * q + 4, :].bitcast(I32), x_scales[0, 4 * q : 4 * q + 4, :].bitcast(I32))
-        nc.sync.dma_start(raw[0][:], w1_rows[:, :, 0:HALF])
-        nc.sync.dma_start(raw[1][:], w1_rows[:, :, HALF : 2 * HALF])
-
-        xgs = keep.tile([P, S], U8, name="xgs", align_bytes=64)
-        xg = keep.tile([P, S], U32, name="xg", align_bytes=64)
-        nc.vector.tensor_copy(xg[:], xw[:].indirect(offsets[:]))
-        nc.vector.tensor_copy(xgs[:, 0:CHUNK], xs[:].indirect(offsets[:, 0 : CHUNK // 16]))
-        nc.vector.tensor_copy(xgs[:, CHUNK:S], xs[:].indirect(offsets[:, CHUNK // 16 : S // 16]))
-        pre = psum.tile([32, PACK, CHUNK], F32, name="pre", tag="res3")
-        for i in range(10):
-            nc.tensor.matmul_mx(
-                out=pre[:, i % PACK, :], lhsT=xg[:, 0:32].bitcast(FP8X4), lhsT_scale=xgs[:, 0:32],
-                rhs=xg[:, 0:CHUNK].bitcast(FP8X4), rhs_scale=xgs[:, 0:CHUNK], start=True, stop=True,
-            )
-        w2s = keep.tile([P, N], U8, name="w2s", tag="scales", align_bytes=64)
-        nc.gpsimd.memset(w2s[:].bitcast(I32), 0)
+        nc.sync.dma_start(xw[:].bitcast(I32), x_words[0].rearrange("p n t -> p (n t)").bitcast(I32))
+        nc.sync.dma_start(raw[1][:], w1_rows[:, 2:4, :])
         for q in range(4):
             nc.sync.dma_start(w2s[32 * q : 32 * q + 4, :].bitcast(I32), w2_scales[0, 4 * q : 4 * q + 4, :].bitcast(I32))
 
-        MH = HALF // PACK
-        grouped = keep.tile([P, PACK, P, PACK], BF16, name="grouped", align_bytes=64)
+        xgs = keep.tile([P, S], U8, name="xgs", align_bytes=64)
+        xg = keep.tile([P, S], U32, name="xg", align_bytes=64)
+        nc.vector.tensor_copy(xgs[:], xs[:].indirect(offsets[:]))
+        nc.vector.tensor_copy(xg[:], xw[:].indirect(offsets[:]))
+
+        low = [keep.tile([P, 1, P, PACK], BF16, name="low%d" % t, align_bytes=64) for t in range(2)]
+        high = keep.tile([P, 2, P, PACK], BF16, name="high", align_bytes=64)
+        grouped = [low[0][:, 0], low[1][:, 0], high[:, 0], high[:, 1]]
         wq = [keep.tile([P, P], U32, name="wq%d" % t, align_bytes=64) for t in range(PACK)]
         ws = [keep.tile([P, P], U8, name="ws%d" % t, align_bytes=64) for t in range(PACK)]
 
-        def cast(copy, a, m0, m1):
-            dst = grouped[:, :, a * MH + m0 : a * MH + m1, :].rearrange("p t m j -> p m j t")
-            src = raw[a][:, :, PACK * m0 : PACK * m1].rearrange("p j (m t) -> p m j t", t=PACK)
+        def cast(copy, u, tile, t0, t1):
+            dst = tile[:, :, :, 2 * u : 2 * u + 2].rearrange("p t m j -> p m j t")
+            src = raw[u][:].rearrange("p j (m t) -> p m j t", t=PACK)[:, :, :, t0:t1]
             copy(dst, src)
 
-        cast(nc.scalar.copy, 0, 0, MH)
+        cast(nc.scalar.copy, 0, low[0], 0, 1)
+        cast(nc.scalar.copy, 0, low[1], 1, 2)
+        cast(nc.scalar.copy, 0, high, 2, 4)
         w2w = keep.tile([P, N], U32, name="w2w", tag="raw0", align_bytes=64)
         nc.sync.dma_start(w2w[:].bitcast(I32), w2_words[0].rearrange("p n t -> p (n t)").bitcast(I32))
-        cast(nc.scalar.copy, 1, 0, 26)
-        cast(nc.vector.tensor_copy, 1, 26, MH)
+        cast(nc.vector.tensor_copy, 1, low[0], 0, 1)
+        cast(nc.vector.tensor_copy, 1, low[1], 1, 2)
+        cast(nc.scalar.copy, 1, high, 2, 4)
 
         h = [keep.tile([P, S], F32, name="h%d" % t, align_bytes=64) for t in range(PACK)]
         mean = [keep.tile([P, 1], F32, name="mean%d" % t) for t in range(PACK)]
         chunks = S // CHUNK
         zi = [keep.tile([P, PACK * CHUNK], BF16, name="zi%d" % c, align_bytes=64) for c in range(chunks)]
-        pairs_one = keep.tile([P, 2, 2 * CHUNK], BF16, name="pairs_one", align_bytes=64)
-        pairs_high = keep.tile([P, 2, 2 * HALF], BF16, name="pairs_high", align_bytes=64)
+        pairs = [keep.tile([P, 2, 2 * HALF], BF16, name="pairs%d" % a, align_bytes=64) for a in range(2)]
         for t in range(PACK):
             nc.vector.quantize_mx(
                 out=wq[t][:].bitcast(FP8X4),
                 scales=ws[t][:],
-                in_=grouped[:, t, :, :].rearrange("p m j -> p (m j)"),
+                in_=grouped[t].rearrange("p m j -> p (m j)"),
             )
-        def first_layer(t, cols, acc):
-            nc.tensor.matmul_mx(
-                out=acc, lhsT=wq[t][:].bitcast(FP8X4), lhsT_scale=ws[t][:],
-                rhs=xg[:, cols].bitcast(FP8X4), rhs_scale=xgs[:, cols], start=True, stop=True,
-            )
-
-        part_mean = keep.tile([P, 1], F32, name="part_mean")
-        part_sum = keep.tile([P, 1], F32, name="part_sum")
-        low = psum.tile([P, HALF], F32, name="low", tag="acc0")
-        high = psum.tile([P, HALF], F32, name="high", tag="res2")
-        first_layer(0, slice(0, HALF), low[:])
-        first_layer(0, slice(HALF, S), high[:])
-        nc.scalar.activation(h[0][:, 0:HALF], low[:], ACT.Relu, scale=1.0 / S, accum_out=part_mean[:])
-        nc.vector.tensor_scalar(
-            out=h[0][:, HALF:S], in0=high[:], scalar1=0.0, scalar2=None, op0=ALU.max, op1=ALU.add, accum_out=part_sum[:]
-        )
-        nc.vector.tensor_scalar(
-            out=mean[0][:], in0=part_sum[:], scalar1=1.0 / S, scalar2=part_mean[:], op0=ALU.mult, op1=ALU.add
-        )
-        for t in range(1, PACK):
-            acc = psum.tile([P, S], F32, name="acc%d" % t, tag="acc%d" % t)
-            first_layer(t, slice(0, S), acc[:])
-            nc.scalar.activation(h[t][:], acc[:], ACT.Relu, scale=1.0 / S, accum_out=mean[t][:])
-        def centre(t, dst, cols):
-            nc.vector.tensor_scalar(
-                out=dst, in0=h[t][:, cols], scalar1=1.0 if t == 0 and cols.start >= HALF else float(S), scalar2=mean[t][:],
-                op0=ALU.mult, op1=ALU.subtract,
-            )
-
         for t in range(PACK):
-            centre(t, zi[0][:, t : PACK * CHUNK : PACK], slice(0, CHUNK))
-            centre(t, pairs_high[:, t // 2, t % 2 : 2 * HALF : 2], slice(HALF, S))
-            centre(t, pairs_one[:, t // 2, t % 2 : 2 * CHUNK : 2], slice(CHUNK, HALF))
-        for t in range(PACK - 3, PACK):
-            spin = psum.tile([32, S], F32, name="spin%d" % t, tag="acc%d" % t)
+            acc = psum.tile([P, S], F32, name="acc%d" % t, tag="acc%d" % t)
             nc.tensor.matmul_mx(
-                out=spin[:], lhsT=wq[0][:, 0:32].bitcast(FP8X4), lhsT_scale=ws[0][:, 0:32],
+                out=acc[:], lhsT=wq[t][:].bitcast(FP8X4), lhsT_scale=ws[t][:],
                 rhs=xg[:].bitcast(FP8X4), rhs_scale=xgs[:], start=True, stop=True,
             )
+            nc.scalar.activation(h[t][:], acc[:], ACT.Relu, scale=1.0 / S, accum_out=mean[t][:])
+
+        for t in range(PACK):
+            for a in range(2):
+                nc.vector.tensor_scalar(
+                    out=pairs[a][:, t // 2, t % 2 : 2 * HALF : 2], in0=h[t][:, a * HALF : (a + 1) * HALF],
+                    scalar1=float(S), scalar2=mean[t][:], op0=ALU.mult, op1=ALU.subtract,
+                )
 
         zq = [keep.tile([P, CHUNK], U32, name="zq%d" % c, align_bytes=64) for c in range(chunks)]
         zs = [keep.tile([P, CHUNK], U8, name="zs%d" % c, align_bytes=64) for c in range(chunks)]
 
-        def weave(copy, c, pairs, first):
+        def weave(copy, c):
+            first = (c % 2) * CHUNK
             dst = zi[c][:].bitcast(F32).rearrange("p (n u) -> p n u", u=2)
-            copy(dst, pairs[:].bitcast(F32)[:, :, first : first + CHUNK].rearrange("p u n -> p n u"))
+            copy(dst, pairs[c // 2][:].bitcast(F32)[:, :, first : first + CHUNK].rearrange("p u n -> p n u"))
 
         def quantize_z(c):
             nc.vector.quantize_mx(out=zq[c][:].bitcast(FP8X4), scales=zs[c][:], in_=zi[c][:])
 
-        weave(nc.scalar.copy, 2, pairs_high, 0)
-        weave(nc.scalar.copy, 3, pairs_high, CHUNK)
-        quantize_z(0)
-        weave(nc.vector.tensor_copy, 1, pairs_one, 0)
-        for c in (2, 1, 3):
+        weave(nc.scalar.copy, 0)
+        weave(nc.vector.tensor_copy, 1)
+        weave(nc.scalar.copy, 2)
+        weave(nc.vector.tensor_copy, 3)
+        for c in (1, 0, 3, 2):
             quantize_z(c)
 
         out_rows = out.rearrange("(m p) n -> p m n", p=P)
@@ -161,15 +133,15 @@ def tile_picked_deepset_relu_p_kernel(tc, x_words, x_scales, w1, w2_words, w2_sc
             copy(o[:], res[:])
             nc.sync.dma_start(out_rows[:, :, c * CHUNK : (c + 1) * CHUNK], o[:])
 
-        def finish_split(c, copies, tags):
+        def finish_split(c, copies, tags, queues):
             for m in range(2):
                 res = psum.tile([P, CHUNK], F32, name="res%d_%d" % (c, m), tag=tags[m])
                 second_layer(c, m, res[:])
                 o = keep.tile([P, CHUNK], F32, name="o%d_%d" % (c, m))
                 copies[m](o[:], res[:])
-                nc.sync.dma_start(out_rows[:, m, c * CHUNK : (c + 1) * CHUNK], o[:])
+                queues[m].dma_start(out_rows[:, m, c * CHUNK : (c + 1) * CHUNK], o[:])
 
-        finish_split(0, (nc.scalar.copy, nc.scalar.copy), ("res0", "acc0"))
-        finish_whole(2, nc.scalar.copy)
-        finish_whole(1, nc.vector.tensor_copy)
-        finish_split(3, (nc.scalar.copy, nc.vector.tensor_copy), ("res3", "acc1"))
+        finish_split(1, (nc.scalar.copy, nc.scalar.copy), ("res1", "acc0"), (nc.sync, nc.sync))
+        finish_whole(0, nc.vector.tensor_copy)
+        finish_whole(3, nc.scalar.copy)
+        finish_split(2, (nc.vector.tensor_copy, nc.scalar.copy), ("res2", "acc1"), (nc.sync, nc.scalar))

@@ -37,40 +37,37 @@ def tile_picked_deepset_relu_p_kernel(tc, x_words, x_scales, w1, w2_words, w2_sc
         nc.vector.memset(w2s[:].bitcast(I32), 0)
 
         w1_rows = w1.rearrange("(p j) c -> p j c", j=PACK)
-        nc.scalar.dma_start(raw[0][:], w1_rows[:, 0:2, :])
+        nc.scalar.dma_start(xw[:].bitcast(I32), x_words[0].rearrange("p n t -> p (n t)").bitcast(I32))
         nc.sync.dma_start(offsets[:], offs)
         for q in range(4):
             queue = nc.sync if q < 2 else nc.scalar
             queue.dma_start(xs[32 * q : 32 * q + 4, :].bitcast(I32), x_scales[0, 4 * q : 4 * q + 4, :].bitcast(I32))
-        nc.sync.dma_start(xw[:].bitcast(I32), x_words[0].rearrange("p n t -> p (n t)").bitcast(I32))
+        nc.sync.dma_start(raw[0][:], w1_rows[:, 0:2, :])
         nc.sync.dma_start(raw[1][:], w1_rows[:, 2:4, :])
         for q in range(4):
             nc.sync.dma_start(w2s[32 * q : 32 * q + 4, :].bitcast(I32), w2_scales[0, 4 * q : 4 * q + 4, :].bitcast(I32))
 
         xgs = keep.tile([P, S], U8, name="xgs", align_bytes=64)
         xg = keep.tile([P, S], U32, name="xg", align_bytes=64)
-        nc.vector.tensor_copy(xgs[:], xs[:].indirect(offsets[:]))
         nc.vector.tensor_copy(xg[:], xw[:].indirect(offsets[:]))
+        nc.vector.tensor_copy(xgs[:], xs[:].indirect(offsets[:]))
 
-        low = [keep.tile([P, 1, P, PACK], BF16, name="low%d" % t, align_bytes=64) for t in range(2)]
-        high = keep.tile([P, 2, P, PACK], BF16, name="high", align_bytes=64)
-        grouped = [low[0][:, 0], low[1][:, 0], high[:, 0], high[:, 1]]
+        grouped = [keep.tile([P, 2, P, PACK], BF16, name="grouped%d" % v, align_bytes=64) for v in range(2)]
         wq = [keep.tile([P, P], U32, name="wq%d" % t, align_bytes=64) for t in range(PACK)]
         ws = [keep.tile([P, P], U8, name="ws%d" % t, align_bytes=64) for t in range(PACK)]
 
-        def cast(copy, u, tile, t0, t1):
-            dst = tile[:, :, :, 2 * u : 2 * u + 2].rearrange("p t m j -> p m j t")
-            src = raw[u][:].rearrange("p j (m t) -> p m j t", t=PACK)[:, :, :, t0:t1]
+        def cast(copy, u, v, m0=0, m1=P):
+            dst = grouped[v][:, :, m0:m1, 2 * u : 2 * u + 2].rearrange("p t m j -> p m j t")
+            src = raw[u][:].rearrange("p j (m t) -> p m j t", t=PACK)[:, m0:m1, :, 2 * v : 2 * v + 2]
             copy(dst, src)
 
-        cast(nc.scalar.copy, 0, low[0], 0, 1)
-        cast(nc.scalar.copy, 0, low[1], 1, 2)
-        cast(nc.scalar.copy, 0, high, 2, 4)
+        cast(nc.scalar.copy, 0, 0)
+        cast(nc.scalar.copy, 0, 1)
         w2w = keep.tile([P, N], U32, name="w2w", tag="raw0", align_bytes=64)
         nc.sync.dma_start(w2w[:].bitcast(I32), w2_words[0].rearrange("p n t -> p (n t)").bitcast(I32))
-        cast(nc.vector.tensor_copy, 1, low[0], 0, 1)
-        cast(nc.vector.tensor_copy, 1, low[1], 1, 2)
-        cast(nc.scalar.copy, 1, high, 2, 4)
+        cast(nc.vector.tensor_copy, 1, 0)
+        cast(nc.vector.tensor_copy, 1, 1, 0, P // 2)
+        cast(nc.scalar.copy, 1, 1, P // 2, P)
 
         h = [keep.tile([P, S], F32, name="h%d" % t, align_bytes=64) for t in range(PACK)]
         mean = [keep.tile([P, 1], F32, name="mean%d" % t) for t in range(PACK)]
@@ -81,7 +78,7 @@ def tile_picked_deepset_relu_p_kernel(tc, x_words, x_scales, w1, w2_words, w2_sc
             nc.vector.quantize_mx(
                 out=wq[t][:].bitcast(FP8X4),
                 scales=ws[t][:],
-                in_=grouped[t].rearrange("p m j -> p (m j)"),
+                in_=grouped[t // 2][:, t % 2, :, :].rearrange("p m j -> p (m j)"),
             )
         for t in range(PACK):
             acc = psum.tile([P, S], F32, name="acc%d" % t, tag="acc%d" % t)
@@ -90,6 +87,12 @@ def tile_picked_deepset_relu_p_kernel(tc, x_words, x_scales, w1, w2_words, w2_sc
                 rhs=xg[:].bitcast(FP8X4), rhs_scale=xgs[:], start=True, stop=True,
             )
             nc.scalar.activation(h[t][:], acc[:], ACT.Relu, scale=1.0 / S, accum_out=mean[t][:])
+
+        spin = psum.tile([32, S], F32, name="spin", tag="res2")
+        nc.tensor.matmul_mx(
+            out=spin[:], lhsT=wq[PACK - 1][:, 0:32].bitcast(FP8X4), lhsT_scale=ws[PACK - 1][:, 0:32],
+            rhs=xg[:].bitcast(FP8X4), rhs_scale=xgs[:], start=True, stop=True,
+        )
 
         for t in range(PACK):
             for a in range(2):

@@ -62,12 +62,13 @@ def tile_picked_deepset_relu_p_kernel(tc, x_words, x_scales, w1, w2_words, w2_sc
             copy(dst, src)
 
         cast(nc.scalar.copy, 0, 0)
-        cast(nc.scalar.copy, 0, 1)
+        cast(nc.scalar.copy, 0, 1, 0, 44)
+        cast(nc.vector.tensor_copy, 1, 0, 0, 84)
+        cast(nc.scalar.copy, 1, 0, 84, P)
+        cast(nc.scalar.copy, 0, 1, 44, P)
         w2w = keep.tile([P, N], U32, name="w2w", tag="raw0", align_bytes=64)
         nc.sync.dma_start(w2w[:].bitcast(I32), w2_words[0].rearrange("p n t -> p (n t)").bitcast(I32))
-        cast(nc.vector.tensor_copy, 1, 0)
         cast(nc.vector.tensor_copy, 1, 1, 0, P // 2)
-        cast(nc.scalar.copy, 1, 1, P // 2, P)
 
         h = [keep.tile([P, S], F32, name="h%d" % t, align_bytes=64) for t in range(PACK)]
         mean = [keep.tile([P, 1], F32, name="mean%d" % t) for t in range(PACK)]
@@ -75,6 +76,8 @@ def tile_picked_deepset_relu_p_kernel(tc, x_words, x_scales, w1, w2_words, w2_sc
         zi = [keep.tile([P, PACK * CHUNK], BF16, name="zi%d" % c, align_bytes=64) for c in range(chunks)]
         pairs = [keep.tile([P, 2, 2 * HALF], BF16, name="pairs%d" % a, align_bytes=64) for a in range(2)]
         for t in range(PACK):
+            if t == 2:
+                cast(nc.vector.tensor_copy, 1, 1, P // 2, P)
             nc.vector.quantize_mx(
                 out=wq[t][:].bitcast(FP8X4),
                 scales=ws[t][:],
@@ -88,7 +91,7 @@ def tile_picked_deepset_relu_p_kernel(tc, x_words, x_scales, w1, w2_words, w2_sc
             )
             nc.scalar.activation(h[t][:], acc[:], ACT.Relu, scale=1.0 / S, accum_out=mean[t][:])
 
-        spin = psum.tile([32, S], F32, name="spin", tag="res2")
+        spin = psum.tile([32, S], F32, name="spin", tag="acc3")
         nc.tensor.matmul_mx(
             out=spin[:], lhsT=wq[PACK - 1][:, 0:32].bitcast(FP8X4), lhsT_scale=ws[PACK - 1][:, 0:32],
             rhs=xg[:].bitcast(FP8X4), rhs_scale=xgs[:], start=True, stop=True,
@@ -145,6 +148,6 @@ def tile_picked_deepset_relu_p_kernel(tc, x_words, x_scales, w1, w2_words, w2_sc
                 queues[m].dma_start(out_rows[:, m, c * CHUNK : (c + 1) * CHUNK], o[:])
 
         finish_split(1, (nc.scalar.copy, nc.scalar.copy), ("res1", "acc0"), (nc.sync, nc.sync))
-        finish_whole(0, nc.vector.tensor_copy)
-        finish_whole(3, nc.scalar.copy)
+        finish_split(0, (nc.scalar.copy, nc.scalar.copy), ("res0", "acc2"), (nc.sync, nc.sync))
+        finish_whole(3, nc.vector.tensor_copy)
         finish_split(2, (nc.vector.tensor_copy, nc.scalar.copy), ("res2", "acc1"), (nc.sync, nc.scalar))

@@ -17,8 +17,15 @@ ALU = mybir.AluOpType
 
 P = 128
 PACK = 4
-HALF = 256
+QUADRANT = 32
+QUADRANTS = P // QUADRANT
+SCALE_ROWS = 4
+GROUP = 16
+HALF = S // 2
 CHUNK = 128
+CHUNKS = S // CHUNK
+VECTOR_COLUMNS = 84
+SCALAR_COLUMNS = P - VECTOR_COLUMNS
 
 
 def tile_picked_deepset_relu_p_kernel(tc, x_words, x_scales, w1, w2_words, w2_scales, offs, out):
@@ -27,7 +34,7 @@ def tile_picked_deepset_relu_p_kernel(tc, x_words, x_scales, w1, w2_words, w2_sc
         keep = ctx.enter_context(tc.tile_pool(name="keep", bufs=1))
         psum = ctx.enter_context(tc.psum_pool(name="psum", bufs=1))
 
-        offsets = keep.tile([P, S // 16], U16, name="offsets")
+        offsets = keep.tile([P, S // GROUP], U16, name="offsets")
         xw = keep.tile([P, T], U32, name="xw", align_bytes=64)
         xs = keep.tile([P, T], U8, name="xs", align_bytes=64)
         w2s = keep.tile([P, N], U8, name="w2s", align_bytes=64)
@@ -36,16 +43,21 @@ def tile_picked_deepset_relu_p_kernel(tc, x_words, x_scales, w1, w2_words, w2_sc
         nc.vector.memset(xs[:].bitcast(I32), 0)
         nc.vector.memset(w2s[:].bitcast(I32), 0)
 
+        def load_scale_rows(queue, tile, scales, q):
+            queue.dma_start(
+                tile[QUADRANT * q : QUADRANT * q + SCALE_ROWS, :].bitcast(I32),
+                scales[0, SCALE_ROWS * q : SCALE_ROWS * (q + 1), :].bitcast(I32),
+            )
+
         w1_rows = w1.rearrange("(p j) c -> p j c", j=PACK)
         nc.scalar.dma_start(xw[:].bitcast(I32), x_words[0].rearrange("p n t -> p (n t)").bitcast(I32))
         nc.sync.dma_start(offsets[:], offs)
-        for q in range(4):
-            queue = nc.sync if q < 2 else nc.scalar
-            queue.dma_start(xs[32 * q : 32 * q + 4, :].bitcast(I32), x_scales[0, 4 * q : 4 * q + 4, :].bitcast(I32))
-        nc.sync.dma_start(raw[0][:], w1_rows[:, 0:2, :])
-        nc.sync.dma_start(raw[1][:], w1_rows[:, 2:4, :])
-        for q in range(4):
-            nc.sync.dma_start(w2s[32 * q : 32 * q + 4, :].bitcast(I32), w2_scales[0, 4 * q : 4 * q + 4, :].bitcast(I32))
+        for q in range(QUADRANTS):
+            load_scale_rows(nc.sync if q < QUADRANTS // 2 else nc.scalar, xs, x_scales, q)
+        for u in range(2):
+            nc.sync.dma_start(raw[u][:], w1_rows[:, 2 * u : 2 * u + 2, :])
+        for q in range(QUADRANTS):
+            load_scale_rows(nc.sync, w2s, w2_scales, q)
 
         xgs = keep.tile([P, S], U8, name="xgs", align_bytes=64)
         xg = keep.tile([P, S], U32, name="xg", align_bytes=64)
@@ -56,33 +68,38 @@ def tile_picked_deepset_relu_p_kernel(tc, x_words, x_scales, w1, w2_words, w2_sc
         wq = [keep.tile([P, P], U32, name="wq%d" % t, align_bytes=64) for t in range(PACK)]
         ws = [keep.tile([P, P], U8, name="ws%d" % t, align_bytes=64) for t in range(PACK)]
 
-        def cast(copy, u, v, m0=0, m1=P):
+        def cast(copy, u, v, m0, m1):
             dst = grouped[v][:, :, m0:m1, 2 * u : 2 * u + 2].rearrange("p t m j -> p m j t")
             src = raw[u][:].rearrange("p j (m t) -> p m j t", t=PACK)[:, m0:m1, :, 2 * v : 2 * v + 2]
             copy(dst, src)
 
-        cast(nc.scalar.copy, 0, 0)
-        cast(nc.scalar.copy, 0, 1, 0, 44)
-        cast(nc.vector.tensor_copy, 1, 0, 0, 84)
-        cast(nc.scalar.copy, 1, 0, 84, P)
-        cast(nc.scalar.copy, 0, 1, 44, P)
+        def quantize_w1(t):
+            nc.vector.quantize_mx(
+                out=wq[t][:].bitcast(FP8X4),
+                scales=ws[t][:],
+                in_=grouped[t // 2][:, t % 2, :, :].rearrange("p m j -> p (m j)"),
+            )
+
+        cast(nc.scalar.copy, 0, 0, 0, P)
+        cast(nc.scalar.copy, 0, 1, 0, SCALAR_COLUMNS)
+        cast(nc.vector.tensor_copy, 1, 0, 0, VECTOR_COLUMNS)
+        cast(nc.scalar.copy, 1, 0, VECTOR_COLUMNS, P)
+        cast(nc.scalar.copy, 0, 1, SCALAR_COLUMNS, P)
         w2w = keep.tile([P, N], U32, name="w2w", tag="raw0", align_bytes=64)
         nc.sync.dma_start(w2w[:].bitcast(I32), w2_words[0].rearrange("p n t -> p (n t)").bitcast(I32))
         cast(nc.vector.tensor_copy, 1, 1, 0, P // 2)
 
         h = [keep.tile([P, S], F32, name="h%d" % t, align_bytes=64) for t in range(PACK)]
         mean = [keep.tile([P, 1], F32, name="mean%d" % t) for t in range(PACK)]
-        chunks = S // CHUNK
-        zi = [keep.tile([P, PACK * CHUNK], BF16, name="zi%d" % c, align_bytes=64) for c in range(chunks)]
+        zi = [keep.tile([P, PACK * CHUNK], BF16, name="zi%d" % c, align_bytes=64) for c in range(CHUNKS)]
         pairs = [keep.tile([P, 2, 2 * HALF], BF16, name="pairs%d" % a, align_bytes=64) for a in range(2)]
-        for t in range(PACK):
-            if t == 2:
-                cast(nc.vector.tensor_copy, 1, 1, P // 2, P)
-            nc.vector.quantize_mx(
-                out=wq[t][:].bitcast(FP8X4),
-                scales=ws[t][:],
-                in_=grouped[t // 2][:, t % 2, :, :].rearrange("p m j -> p (m j)"),
-            )
+
+        quantize_w1(0)
+        quantize_w1(1)
+        cast(nc.vector.tensor_copy, 1, 1, P // 2, P)
+        quantize_w1(2)
+        quantize_w1(3)
+
         for t in range(PACK):
             acc = psum.tile([P, S], F32, name="acc%d" % t, tag="acc%d" % t)
             nc.tensor.matmul_mx(
@@ -91,12 +108,6 @@ def tile_picked_deepset_relu_p_kernel(tc, x_words, x_scales, w1, w2_words, w2_sc
             )
             nc.scalar.activation(h[t][:], acc[:], ACT.Relu, scale=1.0 / S, accum_out=mean[t][:])
 
-        spin = psum.tile([32, S], F32, name="spin", tag="acc3")
-        nc.tensor.matmul_mx(
-            out=spin[:], lhsT=wq[PACK - 1][:, 0:32].bitcast(FP8X4), lhsT_scale=ws[PACK - 1][:, 0:32],
-            rhs=xg[:].bitcast(FP8X4), rhs_scale=xgs[:], start=True, stop=True,
-        )
-
         for t in range(PACK):
             for a in range(2):
                 nc.vector.tensor_scalar(
@@ -104,28 +115,23 @@ def tile_picked_deepset_relu_p_kernel(tc, x_words, x_scales, w1, w2_words, w2_sc
                     scalar1=float(S), scalar2=mean[t][:], op0=ALU.mult, op1=ALU.subtract,
                 )
 
-        zq = [keep.tile([P, CHUNK], U32, name="zq%d" % c, align_bytes=64) for c in range(chunks)]
-        zs = [keep.tile([P, CHUNK], U8, name="zs%d" % c, align_bytes=64) for c in range(chunks)]
+        zq = [keep.tile([P, CHUNK], U32, name="zq%d" % c, align_bytes=64) for c in range(CHUNKS)]
+        zs = [keep.tile([P, CHUNK], U8, name="zs%d" % c, align_bytes=64) for c in range(CHUNKS)]
 
-        def weave(copy, c):
+        for c in range(CHUNKS):
+            copy = nc.vector.tensor_copy if c % 2 else nc.scalar.copy
             first = (c % 2) * CHUNK
-            dst = zi[c][:].bitcast(F32).rearrange("p (n u) -> p n u", u=2)
-            copy(dst, pairs[c // 2][:].bitcast(F32)[:, :, first : first + CHUNK].rearrange("p u n -> p n u"))
-
-        def quantize_z(c):
+            copy(
+                zi[c][:].bitcast(F32).rearrange("p (n v) -> p n v", v=2),
+                pairs[c // 2][:].bitcast(F32)[:, :, first : first + CHUNK].rearrange("p v n -> p n v"),
+            )
+        for c in (1, 0, 3, 2):
             nc.vector.quantize_mx(out=zq[c][:].bitcast(FP8X4), scales=zs[c][:], in_=zi[c][:])
 
-        weave(nc.scalar.copy, 0)
-        weave(nc.vector.tensor_copy, 1)
-        weave(nc.scalar.copy, 2)
-        weave(nc.vector.tensor_copy, 3)
-        for c in (1, 0, 3, 2):
-            quantize_z(c)
+        out_rows = out.rearrange("(r p) n -> p r n", p=P)
 
-        out_rows = out.rearrange("(m p) n -> p m n", p=P)
-
-        def second_layer(c, m, res):
-            rows = slice(m * P, (m + 1) * P)
+        def second_layer(c, r, res):
+            rows = slice(r * P, (r + 1) * P)
             nc.tensor.matmul_mx(
                 out=res, lhsT=w2w[:, rows].bitcast(FP8X4), lhsT_scale=w2s[:, rows],
                 rhs=zq[c][:].bitcast(FP8X4), rhs_scale=zs[c][:], start=True, stop=True,
@@ -133,21 +139,21 @@ def tile_picked_deepset_relu_p_kernel(tc, x_words, x_scales, w1, w2_words, w2_sc
 
         def finish_whole(c, copy):
             res = psum.tile([P, 2, CHUNK], F32, name="res%d" % c, tag="res%d" % c)
-            for m in range(2):
-                second_layer(c, m, res[:, m, :])
-            o = keep.tile([P, 2, CHUNK], F32, name="o%d" % c)
-            copy(o[:], res[:])
-            nc.sync.dma_start(out_rows[:, :, c * CHUNK : (c + 1) * CHUNK], o[:])
+            for r in range(2):
+                second_layer(c, r, res[:, r, :])
+            staged = keep.tile([P, 2, CHUNK], F32, name="o%d" % c)
+            copy(staged[:], res[:])
+            nc.sync.dma_start(out_rows[:, :, c * CHUNK : (c + 1) * CHUNK], staged[:])
 
-        def finish_split(c, copies, tags, queues):
-            for m in range(2):
-                res = psum.tile([P, CHUNK], F32, name="res%d_%d" % (c, m), tag=tags[m])
-                second_layer(c, m, res[:])
-                o = keep.tile([P, CHUNK], F32, name="o%d_%d" % (c, m))
-                copies[m](o[:], res[:])
-                queues[m].dma_start(out_rows[:, m, c * CHUNK : (c + 1) * CHUNK], o[:])
+        def finish_by_parts(c, copies, banks, queues):
+            for r in range(2):
+                res = psum.tile([P, CHUNK], F32, name="res%d_%d" % (c, r), tag=banks[r])
+                second_layer(c, r, res[:])
+                staged = keep.tile([P, CHUNK], F32, name="o%d_%d" % (c, r))
+                copies[r](staged[:], res[:])
+                queues[r].dma_start(out_rows[:, r, c * CHUNK : (c + 1) * CHUNK], staged[:])
 
-        finish_split(1, (nc.scalar.copy, nc.scalar.copy), ("res1", "acc0"), (nc.sync, nc.sync))
-        finish_split(0, (nc.scalar.copy, nc.scalar.copy), ("res0", "acc2"), (nc.sync, nc.sync))
+        finish_by_parts(1, (nc.scalar.copy, nc.scalar.copy), ("res1", "acc0"), (nc.sync, nc.sync))
+        finish_by_parts(0, (nc.scalar.copy, nc.scalar.copy), ("res0", "acc2"), (nc.sync, nc.sync))
         finish_whole(3, nc.vector.tensor_copy)
-        finish_split(2, (nc.vector.tensor_copy, nc.scalar.copy), ("res2", "acc1"), (nc.sync, nc.scalar))
+        finish_by_parts(2, (nc.vector.tensor_copy, nc.scalar.copy), ("res2", "acc1"), (nc.sync, nc.scalar))

@@ -24,8 +24,7 @@ GROUP = 16
 HALF = S // 2
 CHUNK = 128
 CHUNKS = S // CHUNK
-VECTOR_COLUMNS = 84
-SCALAR_COLUMNS = P - VECTOR_COLUMNS
+EARLY_COLUMNS = 44
 
 
 def tile_picked_deepset_relu_p_kernel(tc, x_words, x_scales, w1, w2_words, w2_scales, offs, out):
@@ -81,18 +80,13 @@ def tile_picked_deepset_relu_p_kernel(tc, x_words, x_scales, w1, w2_words, w2_sc
             )
 
         cast(nc.scalar.copy, 0, 0, 0, P)
-        cast(nc.scalar.copy, 0, 1, 0, SCALAR_COLUMNS)
-        cast(nc.vector.tensor_copy, 1, 0, 0, VECTOR_COLUMNS)
-        cast(nc.scalar.copy, 1, 0, VECTOR_COLUMNS, P)
-        cast(nc.scalar.copy, 0, 1, SCALAR_COLUMNS, P)
+        cast(nc.scalar.copy, 0, 1, 0, EARLY_COLUMNS)
+        cast(nc.vector.tensor_copy, 1, 0, 0, P // 2)
+        cast(nc.scalar.copy, 1, 0, P // 2, P)
+        cast(nc.scalar.copy, 0, 1, EARLY_COLUMNS, P)
         w2w = keep.tile([P, N], U32, name="w2w", tag="raw0", align_bytes=64)
         nc.sync.dma_start(w2w[:].bitcast(I32), w2_words[0].rearrange("p n t -> p (n t)").bitcast(I32))
         cast(nc.vector.tensor_copy, 1, 1, 0, P // 2)
-
-        h = [keep.tile([P, S], F32, name="h%d" % t, align_bytes=64) for t in range(PACK)]
-        mean = [keep.tile([P, 1], F32, name="mean%d" % t) for t in range(PACK)]
-        zi = [keep.tile([P, PACK * CHUNK], BF16, name="zi%d" % c, align_bytes=64) for c in range(CHUNKS)]
-        pairs = [keep.tile([P, 2, 2 * HALF], BF16, name="pairs%d" % a, align_bytes=64) for a in range(2)]
 
         quantize_w1(0)
         quantize_w1(1)
@@ -100,19 +94,39 @@ def tile_picked_deepset_relu_p_kernel(tc, x_words, x_scales, w1, w2_words, w2_sc
         quantize_w1(2)
         quantize_w1(3)
 
-        for t in range(PACK):
-            acc = psum.tile([P, S], F32, name="acc%d" % t, tag="acc%d" % t)
+        halves = [slice(a * HALF, (a + 1) * HALF) for a in range(2)]
+        h = [keep.tile([P, S], F32, name="h%d" % t, align_bytes=64) for t in range(PACK)]
+        total = [keep.tile([P, 1], F32, name="total%d" % t) for t in range(PACK)]
+        first_half = [keep.tile([P, 1], F32, name="first_half%d" % t) for t in range(2)]
+        zi = [keep.tile([P, PACK * CHUNK], BF16, name="zi%d" % c, align_bytes=64) for c in range(CHUNKS)]
+        pairs = [keep.tile([P, 2, 2 * HALF], BF16, name="pairs%d" % a, align_bytes=64) for a in range(2)]
+
+        def first_layer(t, members, bank):
+            acc = psum.tile([P, members.stop - members.start], F32, name="acc_" + bank, tag=bank)
             nc.tensor.matmul_mx(
                 out=acc[:], lhsT=wq[t][:].bitcast(FP8X4), lhsT_scale=ws[t][:],
-                rhs=xg[:].bitcast(FP8X4), rhs_scale=xgs[:], start=True, stop=True,
+                rhs=xg[:, members].bitcast(FP8X4), rhs_scale=xgs[:, members], start=True, stop=True,
             )
-            nc.scalar.activation(h[t][:], acc[:], ACT.Relu, scale=1.0 / S, accum_out=mean[t][:])
+            return acc
+
+        for t in range(2):
+            acc = first_layer(t, halves[0], "bank%d" % t)
+            nc.scalar.activation(h[t][:, halves[0]], acc[:], ACT.Relu, accum_out=first_half[t][:])
+        for t in range(2):
+            acc = first_layer(t, halves[1], "bank%d" % (2 + t))
+            nc.vector.tensor_scalar(
+                out=h[t][:, halves[1]], in0=acc[:], scalar1=0.0, scalar2=first_half[t][:],
+                op0=ALU.max, op1=ALU.add, accum_out=total[t][:],
+            )
+        for t in range(2, PACK):
+            acc = first_layer(t, slice(0, S), "bank%d" % (2 + t))
+            nc.scalar.activation(h[t][:], acc[:], ACT.Relu, accum_out=total[t][:])
 
         for t in range(PACK):
             for a in range(2):
                 nc.vector.tensor_scalar(
                     out=pairs[a][:, t // 2, t % 2 : 2 * HALF : 2], in0=h[t][:, a * HALF : (a + 1) * HALF],
-                    scalar1=float(S), scalar2=mean[t][:], op0=ALU.mult, op1=ALU.subtract,
+                    scalar1=float(S), scalar2=total[t][:], op0=ALU.mult, op1=ALU.subtract,
                 )
 
         zq = [keep.tile([P, CHUNK], U32, name="zq%d" % c, align_bytes=64) for c in range(CHUNKS)]
@@ -137,8 +151,14 @@ def tile_picked_deepset_relu_p_kernel(tc, x_words, x_scales, w1, w2_words, w2_sc
                 rhs=zq[c][:].bitcast(FP8X4), rhs_scale=zs[c][:], start=True, stop=True,
             )
 
-        def finish_whole(c, copy):
-            res = psum.tile([P, 2, CHUNK], F32, name="res%d" % c, tag="res%d" % c)
+        def on_scalar(dst, src):
+            nc.scalar.activation(dst, src, ACT.Copy, scale=1.0 / S)
+
+        def on_vector(dst, src):
+            nc.vector.tensor_scalar(out=dst, in0=src, scalar1=1.0 / S, scalar2=None, op0=ALU.mult)
+
+        def finish_whole(c, copy, bank):
+            res = psum.tile([P, 2, CHUNK], F32, name="res%d" % c, tag=bank)
             for r in range(2):
                 second_layer(c, r, res[:, r, :])
             staged = keep.tile([P, 2, CHUNK], F32, name="o%d" % c)
@@ -153,7 +173,7 @@ def tile_picked_deepset_relu_p_kernel(tc, x_words, x_scales, w1, w2_words, w2_sc
                 copies[r](staged[:], res[:])
                 queues[r].dma_start(out_rows[:, r, c * CHUNK : (c + 1) * CHUNK], staged[:])
 
-        finish_by_parts(1, (nc.scalar.copy, nc.scalar.copy), ("res1", "acc0"), (nc.sync, nc.sync))
-        finish_by_parts(0, (nc.scalar.copy, nc.scalar.copy), ("res0", "acc2"), (nc.sync, nc.sync))
-        finish_whole(3, nc.vector.tensor_copy)
-        finish_by_parts(2, (nc.vector.tensor_copy, nc.scalar.copy), ("res2", "acc1"), (nc.sync, nc.scalar))
+        finish_by_parts(1, (on_scalar, on_scalar), ("bank6", "bank7"), (nc.sync, nc.sync))
+        finish_by_parts(0, (on_scalar, on_scalar), ("bank0", "bank1"), (nc.sync, nc.sync))
+        finish_whole(3, on_vector, "bank2")
+        finish_by_parts(2, (on_vector, on_scalar), ("bank3", "bank4"), (nc.sync, nc.scalar))

@@ -122,6 +122,12 @@ def tile_picked_deepset_relu_p_kernel(tc, x_words, x_scales, w1, w2_words, w2_sc
             acc = first_layer(t, slice(0, S), "bank%d" % (2 + t))
             nc.scalar.activation(h[t][:], acc[:], ACT.Relu, accum_out=total[t][:])
 
+        idle = psum.tile([QUADRANT, S], F32, name="idle", tag="bank7")
+        nc.tensor.matmul_mx(
+            out=idle[:], lhsT=wq[3][:, :QUADRANT].bitcast(FP8X4), lhsT_scale=ws[3][:, :QUADRANT],
+            rhs=xg[:].bitcast(FP8X4), rhs_scale=xgs[:], start=True, stop=True,
+        )
+
         for t in range(PACK):
             for a in range(2):
                 nc.vector.tensor_scalar(

@@ -163,14 +163,6 @@ def tile_picked_deepset_relu_p_kernel(tc, x_words, x_scales, w1, w2_words, w2_sc
         def on_vector(dst, src):
             nc.vector.tensor_scalar(out=dst, in0=src, scalar1=1.0 / S, scalar2=None, op0=ALU.mult)
 
-        def finish_whole(c, copy, bank):
-            res = psum.tile([P, 2, CHUNK], F32, name="res%d" % c, tag=bank)
-            for r in range(2):
-                second_layer(c, r, res[:, r, :])
-            staged = keep.tile([P, 2, CHUNK], F32, name="o%d" % c)
-            copy(staged[:], res[:])
-            nc.sync.dma_start(out_rows[:, :, c * CHUNK : (c + 1) * CHUNK], staged[:])
-
         def finish_by_parts(c, copies, banks, queues):
             for r in range(2):
                 res = psum.tile([P, CHUNK], F32, name="res%d_%d" % (c, r), tag=banks[r])
@@ -181,5 +173,11 @@ def tile_picked_deepset_relu_p_kernel(tc, x_words, x_scales, w1, w2_words, w2_sc
 
         finish_by_parts(1, (on_scalar, on_scalar), ("bank6", "bank7"), (nc.sync, nc.sync))
         finish_by_parts(0, (on_scalar, on_scalar), ("bank0", "bank1"), (nc.sync, nc.sync))
-        finish_whole(3, on_vector, "bank2")
-        finish_by_parts(2, (on_vector, on_scalar), ("bank3", "bank4"), (nc.sync, nc.scalar))
+        upper = [psum.tile([P, 2, CHUNK], F32, name="upper%d" % r, tag="bank%d" % (2 + r)) for r in range(2)]
+        for c in (3, 2):
+            for r in range(2):
+                second_layer(c, r, upper[r][:, c - 2, :])
+        for r in range(2):
+            staged = keep.tile([P, HALF], F32, name="upper_out%d" % r)
+            (on_vector, on_scalar)[r](staged[:], upper[r][:].rearrange("p c n -> p (c n)"))
+            (nc.sync, nc.scalar)[r].dma_start(out_rows[:, r, HALF:], staged[:])

@@ -135,8 +135,8 @@ def tile_picked_deepset_relu_p_kernel(tc, x_words, x_scales, w1, w2_words, w2_sc
                     scalar1=float(S), scalar2=total[t][:], op0=ALU.mult, op1=ALU.subtract,
                 )
 
-        zq = [keep.tile([P, CHUNK], U32, name="zq%d" % c, align_bytes=64) for c in range(CHUNKS)]
-        zs = [keep.tile([P, CHUNK], U8, name="zs%d" % c, align_bytes=64) for c in range(CHUNKS)]
+        zq = keep.tile([P, S], U32, name="zq", align_bytes=64)
+        zs = keep.tile([P, S], U8, name="zs", align_bytes=64)
 
         for c in range(CHUNKS):
             copy = nc.vector.tensor_copy if c % 2 else nc.scalar.copy
@@ -146,16 +146,10 @@ def tile_picked_deepset_relu_p_kernel(tc, x_words, x_scales, w1, w2_words, w2_sc
                 pairs[c // 2][:].bitcast(F32)[:, :, first : first + CHUNK].rearrange("p v n -> p n v"),
             )
         for c in (1, 0, 3, 2):
-            nc.vector.quantize_mx(out=zq[c][:].bitcast(FP8X4), scales=zs[c][:], in_=zi[c][:])
+            members = slice(c * CHUNK, (c + 1) * CHUNK)
+            nc.vector.quantize_mx(out=zq[:, members].bitcast(FP8X4), scales=zs[:, members], in_=zi[c][:])
 
         out_rows = out.rearrange("(r p) n -> p r n", p=P)
-
-        def second_layer(c, r, res):
-            rows = slice(r * P, (r + 1) * P)
-            nc.tensor.matmul_mx(
-                out=res, lhsT=w2w[:, rows].bitcast(FP8X4), lhsT_scale=w2s[:, rows],
-                rhs=zq[c][:].bitcast(FP8X4), rhs_scale=zs[c][:], start=True, stop=True,
-            )
 
         def on_scalar(dst, src):
             nc.scalar.activation(dst, src, ACT.Copy, scale=1.0 / S)
@@ -163,21 +157,21 @@ def tile_picked_deepset_relu_p_kernel(tc, x_words, x_scales, w1, w2_words, w2_sc
         def on_vector(dst, src):
             nc.vector.tensor_scalar(out=dst, in0=src, scalar1=1.0 / S, scalar2=None, op0=ALU.mult)
 
-        def finish_by_parts(c, copies, banks, queues):
-            for r in range(2):
-                res = psum.tile([P, CHUNK], F32, name="res%d_%d" % (c, r), tag=banks[r])
-                second_layer(c, r, res[:])
-                staged = keep.tile([P, CHUNK], F32, name="o%d_%d" % (c, r))
-                copies[r](staged[:], res[:])
-                queues[r].dma_start(out_rows[:, r, c * CHUNK : (c + 1) * CHUNK], staged[:])
+        def finish(members, r, bank, copy, queue):
+            name = "%d_%d" % (members.start, r)
+            width = members.stop - members.start
+            rows = slice(r * P, (r + 1) * P)
+            res = psum.tile([P, width], F32, name="res" + name, tag=bank)
+            nc.tensor.matmul_mx(
+                out=res[:], lhsT=w2w[:, rows].bitcast(FP8X4), lhsT_scale=w2s[:, rows],
+                rhs=zq[:, members].bitcast(FP8X4), rhs_scale=zs[:, members], start=True, stop=True,
+            )
+            staged = keep.tile([P, width], F32, name="staged" + name)
+            copy(staged[:], res[:])
+            queue.dma_start(out_rows[:, r, members], staged[:])
 
-        finish_by_parts(1, (on_scalar, on_scalar), ("bank6", "bank7"), (nc.sync, nc.sync))
-        finish_by_parts(0, (on_scalar, on_scalar), ("bank0", "bank1"), (nc.sync, nc.sync))
-        upper = [psum.tile([P, 2, CHUNK], F32, name="upper%d" % r, tag="bank%d" % (2 + r)) for r in range(2)]
-        for c in (3, 2):
+        for c, banks in ((1, ("bank6", "bank7")), (0, ("bank0", "bank1"))):
             for r in range(2):
-                second_layer(c, r, upper[r][:, c - 2, :])
-        for r in range(2):
-            staged = keep.tile([P, HALF], F32, name="upper_out%d" % r)
-            (on_vector, on_scalar)[r](staged[:], upper[r][:].rearrange("p c n -> p (c n)"))
-            (nc.sync, nc.scalar)[r].dma_start(out_rows[:, r, HALF:], staged[:])
+                finish(slice(c * CHUNK, (c + 1) * CHUNK), r, banks[r], on_scalar, nc.sync)
+        finish(halves[1], 0, "bank2", on_vector, nc.sync)
+        finish(halves[1], 1, "bank3", on_scalar, nc.scalar)

@@ -63,6 +63,13 @@ def tile_picked_deepset_relu_p_kernel(tc, x_words, x_scales, w1, w2_words, w2_sc
         nc.vector.tensor_copy(xg[:], xw[:].indirect(offsets[:]))
         nc.vector.tensor_copy(xgs[:], xs[:].indirect(offsets[:]))
 
+        for bank in ("bank6", "bank7"):
+            idle = psum.tile([QUADRANT, S], F32, name="idle_" + bank, tag=bank)
+            nc.tensor.matmul_mx(
+                out=idle[:], lhsT=xg[:, :QUADRANT].bitcast(FP8X4), lhsT_scale=xgs[:, :QUADRANT],
+                rhs=xg[:].bitcast(FP8X4), rhs_scale=xgs[:], start=True, stop=True,
+            )
+
         grouped = [keep.tile([P, 2, P, PACK], BF16, name="grouped%d" % v, align_bytes=64) for v in range(2)]
         wq = [keep.tile([P, P], U32, name="wq%d" % t, align_bytes=64) for t in range(PACK)]
         ws = [keep.tile([P, P], U8, name="ws%d" % t, align_bytes=64) for t in range(PACK)]
@@ -121,12 +128,6 @@ def tile_picked_deepset_relu_p_kernel(tc, x_words, x_scales, w1, w2_words, w2_sc
         for t in range(2, PACK):
             acc = first_layer(t, slice(0, S), "bank%d" % (2 + t))
             nc.scalar.activation(h[t][:], acc[:], ACT.Relu, accum_out=total[t][:])
-
-        idle = psum.tile([QUADRANT, S], F32, name="idle", tag="bank7")
-        nc.tensor.matmul_mx(
-            out=idle[:], lhsT=wq[3][:, :QUADRANT].bitcast(FP8X4), lhsT_scale=ws[3][:, :QUADRANT],
-            rhs=xg[:].bitcast(FP8X4), rhs_scale=xgs[:], start=True, stop=True,
-        )
 
         for t in range(PACK):
             for a in range(2):

@@ -61,14 +61,18 @@ def tile_picked_deepset_relu_p_kernel(tc, x_words, x_scales, w1, w2_words, w2_sc
         xgs = keep.tile([P, S], U8, name="xgs", align_bytes=64)
         xg = keep.tile([P, S], U32, name="xg", align_bytes=64)
         nc.vector.tensor_copy(xg[:], xw[:].indirect(offsets[:]))
-        nc.vector.tensor_copy(xgs[:], xs[:].indirect(offsets[:]))
+        for members in (slice(0, CHUNK), slice(CHUNK, S)):
+            entries = offsets[:, members.start // GROUP : members.stop // GROUP]
+            nc.vector.tensor_copy(xgs[:, members], xs[:].indirect(entries))
 
         for bank in ("bank6", "bank7"):
             idle = psum.tile([QUADRANT, S], F32, name="idle_" + bank, tag=bank)
-            nc.tensor.matmul_mx(
-                out=idle[:], lhsT=xg[:, :QUADRANT].bitcast(FP8X4), lhsT_scale=xgs[:, :QUADRANT],
-                rhs=xg[:].bitcast(FP8X4), rhs_scale=xgs[:], start=True, stop=True,
-            )
+            for c in range(CHUNKS):
+                nc.tensor.matmul_mx(
+                    out=idle[:, c * CHUNK : (c + 1) * CHUNK],
+                    lhsT=xg[:, :QUADRANT].bitcast(FP8X4), lhsT_scale=xgs[:, :QUADRANT],
+                    rhs=xg[:, :CHUNK].bitcast(FP8X4), rhs_scale=xgs[:, :CHUNK], start=True, stop=True,
+                )
 
         grouped = [keep.tile([P, 2, P, PACK], BF16, name="grouped%d" % v, align_bytes=64) for v in range(2)]
         wq = [keep.tile([P, P], U32, name="wq%d" % t, align_bytes=64) for t in range(PACK)]

@@ -24,7 +24,6 @@ GROUP = 16
 HALF = S // 2
 CHUNK = 128
 CHUNKS = S // CHUNK
-EARLY_COLUMNS = 44
 
 
 def tile_picked_deepset_relu_p_kernel(tc, x_words, x_scales, w1, w2_words, w2_scales, offs, out):
@@ -49,21 +48,21 @@ def tile_picked_deepset_relu_p_kernel(tc, x_words, x_scales, w1, w2_words, w2_sc
             )
 
         w1_rows = w1.rearrange("(p j) c -> p j c", j=PACK)
-        nc.scalar.dma_start(xw[:].bitcast(I32), x_words[0].rearrange("p n t -> p (n t)").bitcast(I32))
+        nc.sync.dma_start(raw[0][:], w1_rows[:, 0:2, :])
         nc.sync.dma_start(offsets[:], offs)
         for q in range(QUADRANTS):
-            load_scale_rows(nc.sync if q < QUADRANTS // 2 else nc.scalar, xs, x_scales, q)
-        for u in range(2):
-            nc.sync.dma_start(raw[u][:], w1_rows[:, 2 * u : 2 * u + 2, :])
+            load_scale_rows(nc.sync, xs, x_scales, q)
+        nc.sync.dma_start(xw[:].bitcast(I32), x_words[0].rearrange("p n t -> p (n t)").bitcast(I32))
+        nc.sync.dma_start(raw[1][:], w1_rows[:, 2:4, :])
         for q in range(QUADRANTS):
             load_scale_rows(nc.sync, w2s, w2_scales, q)
 
         xgs = keep.tile([P, S], U8, name="xgs", align_bytes=64)
         xg = keep.tile([P, S], U32, name="xg", align_bytes=64)
-        nc.vector.tensor_copy(xg[:], xw[:].indirect(offsets[:]))
+        nc.vector.tensor_copy(xgs[:], xs[:].indirect(offsets[:]))
         for members in (slice(0, CHUNK), slice(CHUNK, S)):
             entries = offsets[:, members.start // GROUP : members.stop // GROUP]
-            nc.vector.tensor_copy(xgs[:, members], xs[:].indirect(entries))
+            nc.vector.tensor_copy(xg[:, members], xw[:].indirect(entries))
 
         for bank in ("bank6", "bank7"):
             idle = psum.tile([QUADRANT, S], F32, name="idle_" + bank, tag=bank)
@@ -91,24 +90,20 @@ def tile_picked_deepset_relu_p_kernel(tc, x_words, x_scales, w1, w2_words, w2_sc
             )
 
         cast(nc.scalar.copy, 0, 0, 0, P)
-        cast(nc.scalar.copy, 0, 1, 0, EARLY_COLUMNS)
+        cast(nc.scalar.copy, 0, 1, 0, P)
         cast(nc.vector.tensor_copy, 1, 0, 0, P // 2)
         cast(nc.scalar.copy, 1, 0, P // 2, P)
-        cast(nc.scalar.copy, 0, 1, EARLY_COLUMNS, P)
         w2w = keep.tile([P, N], U32, name="w2w", tag="raw0", align_bytes=64)
         nc.sync.dma_start(w2w[:].bitcast(I32), w2_words[0].rearrange("p n t -> p (n t)").bitcast(I32))
         cast(nc.vector.tensor_copy, 1, 1, 0, P // 2)
+        cast(nc.scalar.copy, 1, 1, P // 2, P)
 
-        quantize_w1(0)
-        quantize_w1(1)
-        cast(nc.vector.tensor_copy, 1, 1, P // 2, P)
-        quantize_w1(2)
-        quantize_w1(3)
+        for t in range(PACK):
+            quantize_w1(t)
 
         halves = [slice(a * HALF, (a + 1) * HALF) for a in range(2)]
         h = [keep.tile([P, S], F32, name="h%d" % t, align_bytes=64) for t in range(PACK)]
         total = [keep.tile([P, 1], F32, name="total%d" % t) for t in range(PACK)]
-        first_half = [keep.tile([P, 1], F32, name="first_half%d" % t) for t in range(2)]
         zi = [keep.tile([P, PACK * CHUNK], BF16, name="zi%d" % c, align_bytes=64) for c in range(CHUNKS)]
         pairs = [keep.tile([P, 2, 2 * HALF], BF16, name="pairs%d" % a, align_bytes=64) for a in range(2)]
 
@@ -120,17 +115,12 @@ def tile_picked_deepset_relu_p_kernel(tc, x_words, x_scales, w1, w2_words, w2_sc
             )
             return acc
 
-        for t in range(2):
-            acc = first_layer(t, halves[0], "bank%d" % t)
-            nc.scalar.activation(h[t][:, halves[0]], acc[:], ACT.Relu, accum_out=first_half[t][:])
-        for t in range(2):
-            acc = first_layer(t, halves[1], "bank%d" % (2 + t))
-            nc.vector.tensor_scalar(
-                out=h[t][:, halves[1]], in0=acc[:], scalar1=0.0, scalar2=first_half[t][:],
-                op0=ALU.max, op1=ALU.add, accum_out=total[t][:],
-            )
-        for t in range(2, PACK):
-            acc = first_layer(t, slice(0, S), "bank%d" % (2 + t))
+        acc = first_layer(0, slice(0, S), "bank0")
+        nc.vector.tensor_scalar(
+            out=h[0][:], in0=acc[:], scalar1=0.0, scalar2=None, op0=ALU.max, op1=ALU.add, accum_out=total[0][:],
+        )
+        for t in range(1, PACK):
+            acc = first_layer(t, slice(0, S), "bank%d" % t)
             nc.scalar.activation(h[t][:], acc[:], ACT.Relu, accum_out=total[t][:])
 
         for t in range(PACK):
@@ -175,8 +165,8 @@ def tile_picked_deepset_relu_p_kernel(tc, x_words, x_scales, w1, w2_words, w2_sc
             copy(staged[:], res[:])
             queue.dma_start(out_rows[:, r, members], staged[:])
 
-        for c, banks in ((1, ("bank6", "bank7")), (0, ("bank0", "bank1"))):
+        for c, banks in ((1, ("bank6", "bank7")), (0, ("bank4", "bank5"))):
             for r in range(2):
                 finish(slice(c * CHUNK, (c + 1) * CHUNK), r, banks[r], on_scalar, nc.sync)
-        finish(halves[1], 0, "bank2", on_vector, nc.sync)
-        finish(halves[1], 1, "bank3", on_scalar, nc.scalar)
+        finish(halves[1], 0, "bank0", on_vector, nc.sync)
+        finish(halves[1], 1, "bank1", on_scalar, nc.scalar)

@@ -24,6 +24,7 @@ GROUP = 16
 HALF = S // 2
 CHUNK = 128
 CHUNKS = S // CHUNK
+VECTOR_TILES = (1, 2)
 
 
 def tile_picked_deepset_relu_p_kernel(tc, x_words, x_scales, w1, w2_words, w2_scales, offs, out):
@@ -41,21 +42,20 @@ def tile_picked_deepset_relu_p_kernel(tc, x_words, x_scales, w1, w2_words, w2_sc
         nc.vector.memset(xs[:].bitcast(I32), 0)
         nc.vector.memset(w2s[:].bitcast(I32), 0)
 
-        def load_scale_rows(queue, tile, scales, q):
-            queue.dma_start(
-                tile[QUADRANT * q : QUADRANT * q + SCALE_ROWS, :].bitcast(I32),
-                scales[0, SCALE_ROWS * q : SCALE_ROWS * (q + 1), :].bitcast(I32),
-            )
+        def load_scale_rows(tile, scales):
+            for q in range(QUADRANTS):
+                nc.sync.dma_start(
+                    tile[QUADRANT * q : QUADRANT * q + SCALE_ROWS, :].bitcast(I32),
+                    scales[0, SCALE_ROWS * q : SCALE_ROWS * (q + 1), :].bitcast(I32),
+                )
 
         w1_rows = w1.rearrange("(p j) c -> p j c", j=PACK)
         nc.sync.dma_start(raw[0][:], w1_rows[:, 0:2, :])
         nc.sync.dma_start(offsets[:], offs)
-        for q in range(QUADRANTS):
-            load_scale_rows(nc.sync, xs, x_scales, q)
+        load_scale_rows(xs, x_scales)
         nc.sync.dma_start(xw[:].bitcast(I32), x_words[0].rearrange("p n t -> p (n t)").bitcast(I32))
         nc.sync.dma_start(raw[1][:], w1_rows[:, 2:4, :])
-        for q in range(QUADRANTS):
-            load_scale_rows(nc.sync, w2s, w2_scales, q)
+        load_scale_rows(w2s, w2_scales)
 
         xgs = keep.tile([P, S], U8, name="xgs", align_bytes=64)
         xg = keep.tile([P, S], U32, name="xg", align_bytes=64)
@@ -64,14 +64,16 @@ def tile_picked_deepset_relu_p_kernel(tc, x_words, x_scales, w1, w2_words, w2_sc
             entries = offsets[:, members.start // GROUP : members.stop // GROUP]
             nc.vector.tensor_copy(xg[:, members], xw[:].indirect(entries))
 
-        for bank in ("bank6", "bank7"):
-            idle = psum.tile([QUADRANT, S], F32, name="idle_" + bank, tag=bank)
-            for c in range(CHUNKS):
-                nc.tensor.matmul_mx(
-                    out=idle[:, c * CHUNK : (c + 1) * CHUNK],
-                    lhsT=xg[:, :QUADRANT].bitcast(FP8X4), lhsT_scale=xgs[:, :QUADRANT],
-                    rhs=xg[:, :CHUNK].bitcast(FP8X4), rhs_scale=xgs[:, :CHUNK], start=True, stop=True,
-                )
+        def warm_up(dst, members):
+            nc.tensor.matmul_mx(
+                out=dst, lhsT=xg[:, :QUADRANT].bitcast(FP8X4), lhsT_scale=xgs[:, :QUADRANT],
+                rhs=xg[:, members].bitcast(FP8X4), rhs_scale=xgs[:, members], start=True, stop=True,
+            )
+
+        idle = [psum.tile([QUADRANT, S], F32, name="idle%d" % b, tag="bank%d" % b) for b in (6, 7)]
+        for c in range(CHUNKS):
+            warm_up(idle[0][:, c * CHUNK : (c + 1) * CHUNK], slice(0, CHUNK))
+        warm_up(idle[1][:], slice(0, S))
 
         grouped = [keep.tile([P, 2, P, PACK], BF16, name="grouped%d" % v, align_bytes=64) for v in range(2)]
         wq = [keep.tile([P, P], U32, name="wq%d" % t, align_bytes=64) for t in range(PACK)]
@@ -82,75 +84,83 @@ def tile_picked_deepset_relu_p_kernel(tc, x_words, x_scales, w1, w2_words, w2_sc
             src = raw[u][:].rearrange("p j (m t) -> p m j t", t=PACK)[:, m0:m1, :, 2 * v : 2 * v + 2]
             copy(dst, src)
 
-        def quantize_w1(t):
+        for v in range(2):
+            cast(nc.scalar.copy, 0, v, 0, P)
+        w2w = keep.tile([P, N], U32, name="w2w", tag="raw0", align_bytes=64)
+        nc.sync.dma_start(w2w[:].bitcast(I32), w2_words[0].rearrange("p n t -> p (n t)").bitcast(I32))
+        for v in range(2):
+            cast(nc.vector.tensor_copy, 1, v, 0, P // 2)
+            cast(nc.scalar.copy, 1, v, P // 2, P)
+        for t in range(PACK):
             nc.vector.quantize_mx(
                 out=wq[t][:].bitcast(FP8X4),
                 scales=ws[t][:],
                 in_=grouped[t // 2][:, t % 2, :, :].rearrange("p m j -> p (m j)"),
             )
 
-        cast(nc.scalar.copy, 0, 0, 0, P)
-        cast(nc.scalar.copy, 0, 1, 0, P)
-        cast(nc.vector.tensor_copy, 1, 0, 0, P // 2)
-        cast(nc.scalar.copy, 1, 0, P // 2, P)
-        w2w = keep.tile([P, N], U32, name="w2w", tag="raw0", align_bytes=64)
-        nc.sync.dma_start(w2w[:].bitcast(I32), w2_words[0].rearrange("p n t -> p (n t)").bitcast(I32))
-        cast(nc.vector.tensor_copy, 1, 1, 0, P // 2)
-        cast(nc.scalar.copy, 1, 1, P // 2, P)
-
-        for t in range(PACK):
-            quantize_w1(t)
-
         halves = [slice(a * HALF, (a + 1) * HALF) for a in range(2)]
         h = [keep.tile([P, S], F32, name="h%d" % t, align_bytes=64) for t in range(PACK)]
         total = [keep.tile([P, 1], F32, name="total%d" % t) for t in range(PACK)]
-        zi = [keep.tile([P, PACK * CHUNK], BF16, name="zi%d" % c, align_bytes=64) for c in range(CHUNKS)]
         pairs = [keep.tile([P, 2, 2 * HALF], BF16, name="pairs%d" % a, align_bytes=64) for a in range(2)]
-
-        def first_layer(t, members, bank):
-            acc = psum.tile([P, members.stop - members.start], F32, name="acc_" + bank, tag=bank)
-            nc.tensor.matmul_mx(
-                out=acc[:], lhsT=wq[t][:].bitcast(FP8X4), lhsT_scale=ws[t][:],
-                rhs=xg[:, members].bitcast(FP8X4), rhs_scale=xgs[:, members], start=True, stop=True,
-            )
-            return acc
-
-        acc = first_layer(0, slice(0, S), "bank0")
-        nc.vector.tensor_scalar(
-            out=h[0][:], in0=acc[:], scalar1=0.0, scalar2=None, op0=ALU.max, op1=ALU.add, accum_out=total[0][:],
-        )
-        for t in range(1, PACK):
-            acc = first_layer(t, slice(0, S), "bank%d" % t)
-            nc.scalar.activation(h[t][:], acc[:], ACT.Relu, accum_out=total[t][:])
+        zi = [keep.tile([P, PACK * CHUNK], BF16, name="zi%d" % c, align_bytes=64) for c in range(CHUNKS)]
 
         for t in range(PACK):
-            for a in range(2):
+            acc = psum.tile([P, S], F32, name="acc%d" % t, tag="bank%d" % t)
+            nc.tensor.matmul_mx(
+                out=acc[:], lhsT=wq[t][:].bitcast(FP8X4), lhsT_scale=ws[t][:],
+                rhs=xg[:].bitcast(FP8X4), rhs_scale=xgs[:], start=True, stop=True,
+            )
+            if t in VECTOR_TILES:
                 nc.vector.tensor_scalar(
-                    out=pairs[a][:, t // 2, t % 2 : 2 * HALF : 2], in0=h[t][:, a * HALF : (a + 1) * HALF],
-                    scalar1=float(S), scalar2=total[t][:], op0=ALU.mult, op1=ALU.subtract,
+                    out=h[t][:], in0=acc[:], scalar1=0.0, scalar2=None,
+                    op0=ALU.max, op1=ALU.add, accum_out=total[t][:],
                 )
+            else:
+                nc.scalar.activation(h[t][:], acc[:], ACT.Relu, accum_out=total[t][:])
+
+        def centre(engine, t, a):
+            dst = pairs[a][:, t // 2, t % 2 : 2 * HALF : 2]
+            if engine == "scalar":
+                nc.scalar.activation(dst, h[t][:, halves[a]], ACT.Identity, bias=total[t][:], scale=-float(S))
+            else:
+                (nc.vector if engine == "vector" else nc.gpsimd).tensor_scalar(
+                    out=dst, in0=h[t][:, halves[a]],
+                    scalar1=-float(S), scalar2=total[t][:], op0=ALU.mult, op1=ALU.add,
+                )
+
+        for t in range(2):
+            centre("gpsimd", t, 0)
+            centre("scalar", t, 1)
+        for a in range(2):
+            for t in (3, 2):
+                centre("vector", t, a)
 
         zq = keep.tile([P, S], U32, name="zq", align_bytes=64)
         zs = keep.tile([P, S], U8, name="zs", align_bytes=64)
 
-        for c in range(CHUNKS):
-            copy = nc.vector.tensor_copy if c % 2 else nc.scalar.copy
+        def weave(copy, c):
             first = (c % 2) * CHUNK
             copy(
                 zi[c][:].bitcast(F32).rearrange("p (n v) -> p n v", v=2),
                 pairs[c // 2][:].bitcast(F32)[:, :, first : first + CHUNK].rearrange("p v n -> p n v"),
             )
-        for c in (1, 0, 3, 2):
+
+        def quantize_z(c):
             members = slice(c * CHUNK, (c + 1) * CHUNK)
             nc.vector.quantize_mx(out=zq[:, members].bitcast(FP8X4), scales=zs[:, members], in_=zi[c][:])
+
+        for c in range(CHUNKS):
+            weave(nc.vector.tensor_copy if c % 2 else nc.scalar.copy, c)
+        for c in range(CHUNKS):
+            quantize_z(c)
 
         out_rows = out.rearrange("(r p) n -> p r n", p=P)
 
         def on_scalar(dst, src):
-            nc.scalar.activation(dst, src, ACT.Copy, scale=1.0 / S)
+            nc.scalar.activation(dst, src, ACT.Copy, scale=-1.0 / S)
 
         def on_vector(dst, src):
-            nc.vector.tensor_scalar(out=dst, in0=src, scalar1=1.0 / S, scalar2=None, op0=ALU.mult)
+            nc.vector.tensor_scalar(out=dst, in0=src, scalar1=-1.0 / S, scalar2=None, op0=ALU.mult)
 
         def finish(members, r, bank, copy, queue):
             name = "%d_%d" % (members.start, r)
@@ -165,7 +175,7 @@ def tile_picked_deepset_relu_p_kernel(tc, x_words, x_scales, w1, w2_words, w2_sc
             copy(staged[:], res[:])
             queue.dma_start(out_rows[:, r, members], staged[:])
 
-        for c, banks in ((1, ("bank6", "bank7")), (0, ("bank4", "bank5"))):
+        for c, banks in ((0, ("bank6", "bank7")), (1, ("bank4", "bank5"))):
             for r in range(2):
                 finish(slice(c * CHUNK, (c + 1) * CHUNK), r, banks[r], on_scalar, nc.sync)
         finish(halves[1], 0, "bank0", on_vector, nc.sync)

@@ -24,7 +24,6 @@ GROUP = 16
 HALF = S // 2
 CHUNK = 128
 CHUNKS = S // CHUNK
-VECTOR_TILES = (1, 2)
 
 
 def tile_picked_deepset_relu_p_kernel(tc, x_words, x_scales, w1, w2_words, w2_scales, offs, out):
@@ -88,9 +87,15 @@ def tile_picked_deepset_relu_p_kernel(tc, x_words, x_scales, w1, w2_words, w2_sc
             cast(nc.scalar.copy, 0, v, 0, P)
         w2w = keep.tile([P, N], U32, name="w2w", tag="raw0", align_bytes=64)
         nc.sync.dma_start(w2w[:].bitcast(I32), w2_words[0].rearrange("p n t -> p (n t)").bitcast(I32))
-        for v in range(2):
-            cast(nc.vector.tensor_copy, 1, v, 0, P // 2)
-            cast(nc.scalar.copy, 1, v, P // 2, P)
+        def cast_tile(copy, t, m0, m1):
+            dst = grouped[t // 2][:, t % 2, m0:m1, 2:4]
+            src = raw[1][:].rearrange("p j (m t) -> p m j t", t=PACK)[:, m0:m1, :, t]
+            copy(dst, src)
+
+        cast_tile(nc.vector.tensor_copy, 0, 0, P // 2)
+        cast_tile(nc.scalar.copy, 0, P // 2, P)
+        cast_tile(nc.vector.tensor_copy, 1, 0, P)
+        cast(nc.scalar.copy, 1, 1, 0, P)
         for t in range(PACK):
             nc.vector.quantize_mx(
                 out=wq[t][:].bitcast(FP8X4),
@@ -104,36 +109,32 @@ def tile_picked_deepset_relu_p_kernel(tc, x_words, x_scales, w1, w2_words, w2_sc
         pairs = [keep.tile([P, 2, 2 * HALF], BF16, name="pairs%d" % a, align_bytes=64) for a in range(2)]
         zi = [keep.tile([P, PACK * CHUNK], BF16, name="zi%d" % c, align_bytes=64) for c in range(CHUNKS)]
 
-        for t in range(PACK):
-            acc = psum.tile([P, S], F32, name="acc%d" % t, tag="bank%d" % t)
+        def first_layer(t, members, bank):
+            acc = psum.tile([P, members.stop - members.start], F32, name="acc_" + bank, tag=bank)
             nc.tensor.matmul_mx(
                 out=acc[:], lhsT=wq[t][:].bitcast(FP8X4), lhsT_scale=ws[t][:],
-                rhs=xg[:].bitcast(FP8X4), rhs_scale=xgs[:], start=True, stop=True,
+                rhs=xg[:, members].bitcast(FP8X4), rhs_scale=xgs[:, members], start=True, stop=True,
             )
-            if t in VECTOR_TILES:
+            return acc
+
+        lower = keep.tile([P, 1], F32, name="lower")
+        acc = first_layer(0, halves[0], "bank0")
+        nc.scalar.activation(h[0][:, halves[0]], acc[:], ACT.Relu, accum_out=lower[:])
+        acc = first_layer(0, halves[1], "bank4")
+        nc.vector.tensor_scalar(
+            out=h[0][:, halves[1]], in0=acc[:], scalar1=0.0, scalar2=lower[:],
+            op0=ALU.max, op1=ALU.add, accum_out=total[0][:],
+        )
+        for t in range(1, PACK):
+            acc = first_layer(t, slice(0, S), "bank%d" % t)
+            nc.scalar.activation(h[t][:], acc[:], ACT.Relu, accum_out=total[t][:])
+
+        for t in range(PACK):
+            for a in range(2):
                 nc.vector.tensor_scalar(
-                    out=h[t][:], in0=acc[:], scalar1=0.0, scalar2=None,
-                    op0=ALU.max, op1=ALU.add, accum_out=total[t][:],
+                    out=pairs[a][:, t // 2, t % 2 : 2 * HALF : 2], in0=h[t][:, halves[a]],
+                    scalar1=float(S), scalar2=total[t][:], op0=ALU.mult, op1=ALU.subtract,
                 )
-            else:
-                nc.scalar.activation(h[t][:], acc[:], ACT.Relu, accum_out=total[t][:])
-
-        def centre(engine, t, a):
-            dst = pairs[a][:, t // 2, t % 2 : 2 * HALF : 2]
-            if engine == "scalar":
-                nc.scalar.activation(dst, h[t][:, halves[a]], ACT.Identity, bias=total[t][:], scale=-float(S))
-            else:
-                (nc.vector if engine == "vector" else nc.gpsimd).tensor_scalar(
-                    out=dst, in0=h[t][:, halves[a]],
-                    scalar1=-float(S), scalar2=total[t][:], op0=ALU.mult, op1=ALU.add,
-                )
-
-        for t in range(2):
-            centre("gpsimd", t, 0)
-            centre("scalar", t, 1)
-        for a in range(2):
-            for t in (3, 2):
-                centre("vector", t, a)
 
         zq = keep.tile([P, S], U32, name="zq", align_bytes=64)
         zs = keep.tile([P, S], U8, name="zs", align_bytes=64)
@@ -151,16 +152,16 @@ def tile_picked_deepset_relu_p_kernel(tc, x_words, x_scales, w1, w2_words, w2_sc
 
         for c in range(CHUNKS):
             weave(nc.vector.tensor_copy if c % 2 else nc.scalar.copy, c)
-        for c in range(CHUNKS):
+        for c in (1, 0, 3, 2):
             quantize_z(c)
 
         out_rows = out.rearrange("(r p) n -> p r n", p=P)
 
         def on_scalar(dst, src):
-            nc.scalar.activation(dst, src, ACT.Copy, scale=-1.0 / S)
+            nc.scalar.activation(dst, src, ACT.Copy, scale=1.0 / S)
 
         def on_vector(dst, src):
-            nc.vector.tensor_scalar(out=dst, in0=src, scalar1=-1.0 / S, scalar2=None, op0=ALU.mult)
+            nc.vector.tensor_scalar(out=dst, in0=src, scalar1=1.0 / S, scalar2=None, op0=ALU.mult)
 
         def finish(members, r, bank, copy, queue):
             name = "%d_%d" % (members.start, r)
@@ -175,7 +176,7 @@ def tile_picked_deepset_relu_p_kernel(tc, x_words, x_scales, w1, w2_words, w2_sc
             copy(staged[:], res[:])
             queue.dma_start(out_rows[:, r, members], staged[:])
 
-        for c, banks in ((0, ("bank6", "bank7")), (1, ("bank4", "bank5"))):
+        for c, banks in ((1, ("bank6", "bank7")), (0, ("bank4", "bank5"))):
             for r in range(2):
                 finish(slice(c * CHUNK, (c + 1) * CHUNK), r, banks[r], on_scalar, nc.sync)
         finish(halves[1], 0, "bank0", on_vector, nc.sync)

@@ -24,6 +24,7 @@ GROUP = 16
 HALF = S // 2
 CHUNK = 128
 CHUNKS = S // CHUNK
+CUT = H + H // 2
 
 
 def tile_picked_deepset_relu_p_kernel(tc, x_words, x_scales, w1, w2_words, w2_scales, offs, out):
@@ -36,7 +37,8 @@ def tile_picked_deepset_relu_p_kernel(tc, x_words, x_scales, w1, w2_words, w2_sc
         xw = keep.tile([P, T], U32, name="xw", align_bytes=64)
         xs = keep.tile([P, T], U8, name="xs", align_bytes=64)
         w2s = keep.tile([P, N], U8, name="w2s", align_bytes=64)
-        raw = [keep.tile([P, 2, H], F32, name="raw%d" % u, tag="raw%d" % u, align_bytes=64) for u in range(2)]
+        early = keep.tile([P, CUT], F32, name="early", tag="early", align_bytes=64)
+        late = keep.tile([P, PACK * H - CUT], F32, name="late", align_bytes=64)
 
         nc.vector.memset(xs[:].bitcast(I32), 0)
         nc.vector.memset(w2s[:].bitcast(I32), 0)
@@ -48,12 +50,12 @@ def tile_picked_deepset_relu_p_kernel(tc, x_words, x_scales, w1, w2_words, w2_sc
                     scales[0, SCALE_ROWS * q : SCALE_ROWS * (q + 1), :].bitcast(I32),
                 )
 
-        w1_rows = w1.rearrange("(p j) c -> p j c", j=PACK)
-        nc.sync.dma_start(raw[0][:], w1_rows[:, 0:2, :])
+        w1_rows = w1.rearrange("(p j) c -> p (j c)", j=PACK)
+        nc.sync.dma_start(early[:], w1_rows[:, :CUT])
         nc.sync.dma_start(offsets[:], offs)
         load_scale_rows(xs, x_scales)
         nc.sync.dma_start(xw[:].bitcast(I32), x_words[0].rearrange("p n t -> p (n t)").bitcast(I32))
-        nc.sync.dma_start(raw[1][:], w1_rows[:, 2:4, :])
+        nc.sync.dma_start(late[:], w1_rows[:, CUT:])
         load_scale_rows(w2s, w2_scales)
 
         xgs = keep.tile([P, S], U8, name="xgs", align_bytes=64)
@@ -70,32 +72,37 @@ def tile_picked_deepset_relu_p_kernel(tc, x_words, x_scales, w1, w2_words, w2_sc
             )
 
         idle = [psum.tile([QUADRANT, S], F32, name="idle%d" % b, tag="bank%d" % b) for b in (6, 7)]
-        for c in range(CHUNKS):
-            warm_up(idle[0][:, c * CHUNK : (c + 1) * CHUNK], slice(0, CHUNK))
-        warm_up(idle[1][:], slice(0, S))
+        for bank in idle:
+            for c in range(CHUNKS):
+                warm_up(bank[:, c * CHUNK : (c + 1) * CHUNK], slice(0, CHUNK))
 
         grouped = [keep.tile([P, 2, P, PACK], BF16, name="grouped%d" % v, align_bytes=64) for v in range(2)]
         wq = [keep.tile([P, P], U32, name="wq%d" % t, align_bytes=64) for t in range(PACK)]
         ws = [keep.tile([P, P], U8, name="ws%d" % t, align_bytes=64) for t in range(PACK)]
 
-        def cast(copy, u, v, m0, m1):
-            dst = grouped[v][:, :, m0:m1, 2 * u : 2 * u + 2].rearrange("p t m j -> p m j t")
-            src = raw[u][:].rearrange("p j (m t) -> p m j t", t=PACK)[:, m0:m1, :, 2 * v : 2 * v + 2]
-            copy(dst, src)
+        def cast(copy, piece, side, t0, t1):
+            split = 2 - side
+            j0, j1 = (0, split) if piece == 0 else (split, PACK)
+            source, start = (early, 0) if piece == 0 else (late, CUT)
+            first = 2 * j0 + side - start // (H // 2)
+            half_rows = source[:].rearrange("p (r m t) -> p m r t", m=P // 2, t=PACK)
+            columns = slice(side * (P // 2), (side + 1) * (P // 2))
+            dst = grouped[t0 // 2][:, t0 % 2 : t0 % 2 + t1 - t0, columns, j0:j1].rearrange("p t m j -> p m j t")
+            copy(dst, half_rows[:, :, first : first + 2 * (j1 - j0) - 1 : 2, t0:t1])
 
-        for v in range(2):
-            cast(nc.scalar.copy, 0, v, 0, P)
-        w2w = keep.tile([P, N], U32, name="w2w", tag="raw0", align_bytes=64)
+        cast(nc.vector.tensor_copy, 0, 1, 0, 2)
+        cast(nc.scalar.copy, 0, 0, 0, 2)
+        cast(nc.scalar.copy, 0, 0, 2, 4)
+        cast(nc.scalar.copy, 0, 1, 2, 4)
+        w2w = keep.tile([P, N], U32, name="w2w", tag="early", align_bytes=64)
         nc.sync.dma_start(w2w[:].bitcast(I32), w2_words[0].rearrange("p n t -> p (n t)").bitcast(I32))
-        def cast_tile(copy, t, m0, m1):
-            dst = grouped[t // 2][:, t % 2, m0:m1, 2:4]
-            src = raw[1][:].rearrange("p j (m t) -> p m j t", t=PACK)[:, m0:m1, :, t]
-            copy(dst, src)
 
-        cast_tile(nc.vector.tensor_copy, 0, 0, P // 2)
-        cast_tile(nc.scalar.copy, 0, P // 2, P)
-        cast_tile(nc.vector.tensor_copy, 1, 0, P)
-        cast(nc.scalar.copy, 1, 1, 0, P)
+        cast(nc.vector.tensor_copy, 1, 1, 0, 1)
+        cast(nc.scalar.copy, 1, 0, 0, 1)
+        cast(nc.vector.tensor_copy, 1, 1, 1, 2)
+        cast(nc.vector.tensor_copy, 1, 0, 1, 2)
+        cast(nc.scalar.copy, 1, 0, 2, 4)
+        cast(nc.scalar.copy, 1, 1, 2, 4)
         for t in range(PACK):
             nc.vector.quantize_mx(
                 out=wq[t][:].bitcast(FP8X4),

@@ -72,9 +72,9 @@ def tile_picked_deepset_relu_p_kernel(tc, x_words, x_scales, w1, w2_words, w2_sc
             )
 
         idle = [psum.tile([QUADRANT, S], F32, name="idle%d" % b, tag="bank%d" % b) for b in (6, 7)]
-        for bank in idle:
-            for c in range(CHUNKS):
-                warm_up(bank[:, c * CHUNK : (c + 1) * CHUNK], slice(0, CHUNK))
+        for c in range(CHUNKS):
+            warm_up(idle[0][:, c * CHUNK : (c + 1) * CHUNK], slice(0, CHUNK))
+        warm_up(idle[1][:], slice(0, S))
 
         grouped = [keep.tile([P, 2, P, PACK], BF16, name="grouped%d" % v, align_bytes=64) for v in range(2)]
         wq = [keep.tile([P, P], U32, name="wq%d" % t, align_bytes=64) for t in range(PACK)]

@@ -116,32 +116,32 @@ def tile_picked_deepset_relu_p_kernel(tc, x_words, x_scales, w1, w2_words, w2_sc
         pairs = [keep.tile([P, 2, 2 * HALF], BF16, name="pairs%d" % a, align_bytes=64) for a in range(2)]
         zi = [keep.tile([P, PACK * CHUNK], BF16, name="zi%d" % c, align_bytes=64) for c in range(CHUNKS)]
 
-        def first_layer(t, members, bank):
-            acc = psum.tile([P, members.stop - members.start], F32, name="acc_" + bank, tag=bank)
+        for t in range(PACK):
+            acc = psum.tile([P, S], F32, name="acc%d" % t, tag="bank%d" % t)
             nc.tensor.matmul_mx(
                 out=acc[:], lhsT=wq[t][:].bitcast(FP8X4), lhsT_scale=ws[t][:],
-                rhs=xg[:, members].bitcast(FP8X4), rhs_scale=xgs[:, members], start=True, stop=True,
+                rhs=xg[:].bitcast(FP8X4), rhs_scale=xgs[:], start=True, stop=True,
             )
-            return acc
-
-        lower = keep.tile([P, 1], F32, name="lower")
-        acc = first_layer(0, halves[0], "bank0")
-        nc.scalar.activation(h[0][:, halves[0]], acc[:], ACT.Relu, accum_out=lower[:])
-        acc = first_layer(0, halves[1], "bank4")
-        nc.vector.tensor_scalar(
-            out=h[0][:, halves[1]], in0=acc[:], scalar1=0.0, scalar2=lower[:],
-            op0=ALU.max, op1=ALU.add, accum_out=total[0][:],
-        )
-        for t in range(1, PACK):
-            acc = first_layer(t, slice(0, S), "bank%d" % t)
-            nc.scalar.activation(h[t][:], acc[:], ACT.Relu, accum_out=total[t][:])
-
-        for t in range(PACK):
-            for a in range(2):
+            if t == 1:
                 nc.vector.tensor_scalar(
-                    out=pairs[a][:, t // 2, t % 2 : 2 * HALF : 2], in0=h[t][:, halves[a]],
-                    scalar1=float(S), scalar2=total[t][:], op0=ALU.mult, op1=ALU.subtract,
+                    out=h[t][:], in0=acc[:], scalar1=0.0, scalar2=None,
+                    op0=ALU.max, op1=ALU.add, accum_out=total[t][:],
                 )
+            else:
+                nc.scalar.activation(h[t][:], acc[:], ACT.Relu, accum_out=total[t][:])
+
+        def centre(t, a):
+            nc.vector.tensor_scalar(
+                out=pairs[a][:, t // 2, t % 2 : 2 * HALF : 2], in0=h[t][:, halves[a]],
+                scalar1=float(S), scalar2=total[t][:], op0=ALU.mult, op1=ALU.subtract,
+            )
+
+        for t in range(2):
+            for a in range(2):
+                centre(t, a)
+        for a in range(2):
+            for t in range(2, PACK):
+                centre(t, a)
 
         zq = keep.tile([P, S], U32, name="zq", align_bytes=64)
         zs = keep.tile([P, S], U8, name="zs", align_bytes=64)
@@ -159,7 +159,7 @@ def tile_picked_deepset_relu_p_kernel(tc, x_words, x_scales, w1, w2_words, w2_sc
 
         for c in range(CHUNKS):
             weave(nc.vector.tensor_copy if c % 2 else nc.scalar.copy, c)
-        for c in (1, 0, 3, 2):
+        for c in range(CHUNKS):
             quantize_z(c)
 
         out_rows = out.rearrange("(r p) n -> p r n", p=P)
@@ -183,7 +183,7 @@ def tile_picked_deepset_relu_p_kernel(tc, x_words, x_scales, w1, w2_words, w2_sc
             copy(staged[:], res[:])
             queue.dma_start(out_rows[:, r, members], staged[:])
 
-        for c, banks in ((1, ("bank6", "bank7")), (0, ("bank4", "bank5"))):
+        for c, banks in ((0, ("bank6", "bank7")), (1, ("bank4", "bank5"))):
             for r in range(2):
                 finish(slice(c * CHUNK, (c + 1) * CHUNK), r, banks[r], on_scalar, nc.sync)
         finish(halves[1], 0, "bank0", on_vector, nc.sync)

@@ -116,19 +116,30 @@ def tile_picked_deepset_relu_p_kernel(tc, x_words, x_scales, w1, w2_words, w2_sc
         pairs = [keep.tile([P, 2, 2 * HALF], BF16, name="pairs%d" % a, align_bytes=64) for a in range(2)]
         zi = [keep.tile([P, PACK * CHUNK], BF16, name="zi%d" % c, align_bytes=64) for c in range(CHUNKS)]
 
-        for t in range(PACK):
-            acc = psum.tile([P, S], F32, name="acc%d" % t, tag="bank%d" % t)
-            nc.tensor.matmul_mx(
-                out=acc[:], lhsT=wq[t][:].bitcast(FP8X4), lhsT_scale=ws[t][:],
-                rhs=xg[:].bitcast(FP8X4), rhs_scale=xgs[:], start=True, stop=True,
-            )
-            if t == 1:
-                nc.vector.tensor_scalar(
-                    out=h[t][:], in0=acc[:], scalar1=0.0, scalar2=None,
-                    op0=ALU.max, op1=ALU.add, accum_out=total[t][:],
+        def first_layer(t, spans, bank):
+            first = spans[0].start
+            acc = psum.tile([P, spans[-1].stop - first], F32, name="acc_" + bank, tag=bank)
+            for members in spans:
+                nc.tensor.matmul_mx(
+                    out=acc[:, members.start - first : members.stop - first],
+                    lhsT=wq[t][:].bitcast(FP8X4), lhsT_scale=ws[t][:],
+                    rhs=xg[:, members].bitcast(FP8X4), rhs_scale=xgs[:, members], start=True, stop=True,
                 )
-            else:
-                nc.scalar.activation(h[t][:], acc[:], ACT.Relu, accum_out=total[t][:])
+            return acc
+
+        head = keep.tile([P, 1], F32, name="head")
+        acc = first_layer(0, [slice(0, CHUNK)], "bank4")
+        nc.scalar.activation(h[0][:, :CHUNK], acc[:], ACT.Relu, accum_out=head[:])
+        acc = first_layer(1, [slice(0, S)], "bank1")
+        nc.scalar.activation(h[1][:], acc[:], ACT.Relu, accum_out=total[1][:])
+        acc = first_layer(0, [slice(CHUNK, HALF), halves[1]], "bank0")
+        nc.vector.tensor_scalar(
+            out=h[0][:, CHUNK:], in0=acc[:], scalar1=0.0, scalar2=head[:],
+            op0=ALU.max, op1=ALU.add, accum_out=total[0][:],
+        )
+        for t in range(2, PACK):
+            acc = first_layer(t, [slice(0, S)], "bank%d" % t)
+            nc.scalar.activation(h[t][:], acc[:], ACT.Relu, accum_out=total[t][:])
 
         def centre(t, a):
             nc.vector.tensor_scalar(
@@ -136,7 +147,7 @@ def tile_picked_deepset_relu_p_kernel(tc, x_words, x_scales, w1, w2_words, w2_sc
                 scalar1=float(S), scalar2=total[t][:], op0=ALU.mult, op1=ALU.subtract,
             )
 
-        for t in range(2):
+        for t in (1, 0):
             for a in range(2):
                 centre(t, a)
         for a in range(2):

@@ -181,21 +181,25 @@ def tile_picked_deepset_relu_p_kernel(tc, x_words, x_scales, w1, w2_words, w2_sc
         def on_vector(dst, src):
             nc.vector.tensor_scalar(out=dst, in0=src, scalar1=1.0 / S, scalar2=None, op0=ALU.mult)
 
-        def finish(members, r, bank, copy, queue):
-            name = "%d_%d" % (members.start, r)
-            width = members.stop - members.start
+        def product(dst, members, r):
             rows = slice(r * P, (r + 1) * P)
-            res = psum.tile([P, width], F32, name="res" + name, tag=bank)
             nc.tensor.matmul_mx(
-                out=res[:], lhsT=w2w[:, rows].bitcast(FP8X4), lhsT_scale=w2s[:, rows],
+                out=dst, lhsT=w2w[:, rows].bitcast(FP8X4), lhsT_scale=w2s[:, rows],
                 rhs=zq[:, members].bitcast(FP8X4), rhs_scale=zs[:, members], start=True, stop=True,
             )
-            staged = keep.tile([P, width], F32, name="staged" + name)
-            copy(staged[:], res[:])
-            queue.dma_start(out_rows[:, r, members], staged[:])
 
-        for c, banks in ((0, ("bank6", "bank7")), (1, ("bank4", "bank5"))):
+        for c in range(2):
+            members = slice(c * CHUNK, (c + 1) * CHUNK)
+            res = psum.tile([P, 2 * CHUNK], F32, name="res%d" % c, tag="bank%d" % (6 + c))
             for r in range(2):
-                finish(slice(c * CHUNK, (c + 1) * CHUNK), r, banks[r], on_scalar, nc.sync)
-        finish(halves[1], 0, "bank0", on_vector, nc.sync)
-        finish(halves[1], 1, "bank1", on_scalar, nc.scalar)
+                product(res[:, r * CHUNK : (r + 1) * CHUNK], members, r)
+            staged = keep.tile([P, 2 * CHUNK], F32, name="staged%d" % c)
+            on_scalar(staged[:], res[:])
+            nc.sync.dma_start(out_rows[:, :, members], staged[:].rearrange("p (r n) -> p r n", r=2))
+
+        staged = keep.tile([P, 2 * HALF], F32, name="staged_upper")
+        for r, copy in enumerate((on_vector, on_scalar)):
+            res = psum.tile([P, HALF], F32, name="res_upper%d" % r, tag="bank%d" % r)
+            product(res[:], halves[1], r)
+            copy(staged[:, r * HALF : (r + 1) * HALF], res[:])
+        nc.sync.dma_start(out_rows[:, :, halves[1]], staged[:].rearrange("p (r n) -> p r n", r=2))

@@ -113,7 +113,7 @@ def tile_picked_deepset_relu_p_kernel(tc, x_words, x_scales, w1, w2_words, w2_sc
         halves = [slice(a * HALF, (a + 1) * HALF) for a in range(2)]
         h = [keep.tile([P, S], F32, name="h%d" % t, align_bytes=64) for t in range(PACK)]
         total = [keep.tile([P, 1], F32, name="total%d" % t) for t in range(PACK)]
-        pairs = [keep.tile([P, 2, 2 * HALF], BF16, name="pairs%d" % a, align_bytes=64) for a in range(2)]
+        pairs = [keep.tile([P, 2, 2, CHUNK, 2], BF16, name="pairs%d" % a, align_bytes=64) for a in range(2)]
         zi = [keep.tile([P, PACK * CHUNK], BF16, name="zi%d" % c, align_bytes=64) for c in range(CHUNKS)]
 
         def first_layer(t, spans, bank):
@@ -141,45 +141,52 @@ def tile_picked_deepset_relu_p_kernel(tc, x_words, x_scales, w1, w2_words, w2_sc
             acc = first_layer(t, [slice(0, S)], "bank%d" % t)
             nc.scalar.activation(h[t][:], acc[:], ACT.Relu, accum_out=total[t][:])
 
-        def centre(t, a):
+        def chunks_of(t, c0, c1):
+            src = h[t][:, c0 * CHUNK : c1 * CHUNK].rearrange("p (b n) -> p b n", n=CHUNK)
+            return pairs[c0 // 2][:, c0 % 2 : c0 % 2 + c1 - c0, t // 2, :, t % 2], src
+
+        def centre(t, c0, c1):
+            dst, src = chunks_of(t, c0, c1)
             nc.vector.tensor_scalar(
-                out=pairs[a][:, t // 2, t % 2 : 2 * HALF : 2], in0=h[t][:, halves[a]],
-                scalar1=float(S), scalar2=total[t][:], op0=ALU.mult, op1=ALU.subtract,
+                out=dst, in0=src, scalar1=-float(S), scalar2=total[t][:], op0=ALU.mult, op1=ALU.add
             )
+
+        def centre_on_scalar(t, c):
+            dst, src = chunks_of(t, c, c + 1)
+            nc.scalar.activation(dst, src, ACT.Identity, scale=-float(S), bias=total[t][:])
 
         for t in (1, 0):
             for a in range(2):
-                centre(t, a)
-        for a in range(2):
-            for t in range(2, PACK):
-                centre(t, a)
+                centre(t, 2 * a, 2 * a + 2)
+        for t in range(2, PACK):
+            centre(t, 0, 2)
+        for t in range(2, PACK):
+            centre(t, 2, 3)
+            centre_on_scalar(t, 3)
 
         zq = keep.tile([P, S], U32, name="zq", align_bytes=64)
         zs = keep.tile([P, S], U8, name="zs", align_bytes=64)
 
         def weave(copy, c):
-            first = (c % 2) * CHUNK
-            copy(
-                zi[c][:].bitcast(F32).rearrange("p (n v) -> p n v", v=2),
-                pairs[c // 2][:].bitcast(F32)[:, :, first : first + CHUNK].rearrange("p v n -> p n v"),
-            )
+            words = pairs[c // 2][:, c % 2, :, :, :].rearrange("p v n e -> p v (n e)").bitcast(F32)
+            copy(zi[c][:].bitcast(F32).rearrange("p (n v) -> p n v", v=2), words.rearrange("p v n -> p n v"))
 
         def quantize_z(c):
             members = slice(c * CHUNK, (c + 1) * CHUNK)
             nc.vector.quantize_mx(out=zq[:, members].bitcast(FP8X4), scales=zs[:, members], in_=zi[c][:])
 
         for c in range(CHUNKS):
-            weave(nc.vector.tensor_copy if c % 2 else nc.scalar.copy, c)
+            weave(nc.scalar.copy if c % 2 else nc.vector.tensor_copy, c)
         for c in range(CHUNKS):
             quantize_z(c)
 
         out_rows = out.rearrange("(r p) n -> p r n", p=P)
 
         def on_scalar(dst, src):
-            nc.scalar.activation(dst, src, ACT.Copy, scale=1.0 / S)
+            nc.scalar.activation(dst, src, ACT.Copy, scale=-1.0 / S)
 
         def on_vector(dst, src):
-            nc.vector.tensor_scalar(out=dst, in0=src, scalar1=1.0 / S, scalar2=None, op0=ALU.mult)
+            nc.vector.tensor_scalar(out=dst, in0=src, scalar1=-1.0 / S, scalar2=None, op0=ALU.mult)
 
         def product(dst, members, r):
             rows = slice(r * P, (r + 1) * P)
@@ -188,18 +195,21 @@ def tile_picked_deepset_relu_p_kernel(tc, x_words, x_scales, w1, w2_words, w2_sc
                 rhs=zq[:, members].bitcast(FP8X4), rhs_scale=zs[:, members], start=True, stop=True,
             )
 
-        for c in range(2):
-            members = slice(c * CHUNK, (c + 1) * CHUNK)
-            res = psum.tile([P, 2 * CHUNK], F32, name="res%d" % c, tag="bank%d" % (6 + c))
+        def by_parts(c, dst, banks):
             for r in range(2):
-                product(res[:, r * CHUNK : (r + 1) * CHUNK], members, r)
-            staged = keep.tile([P, 2 * CHUNK], F32, name="staged%d" % c)
-            on_scalar(staged[:], res[:])
-            nc.sync.dma_start(out_rows[:, :, members], staged[:].rearrange("p (r n) -> p r n", r=2))
+                res = psum.tile([P, CHUNK], F32, name="res%d_%d" % (c, r), tag=banks[r])
+                product(res[:], slice(c * CHUNK, (c + 1) * CHUNK), r)
+                on_scalar(dst[:, r, :], res[:])
 
-        staged = keep.tile([P, 2 * HALF], F32, name="staged_upper")
-        for r, copy in enumerate((on_vector, on_scalar)):
-            res = psum.tile([P, HALF], F32, name="res_upper%d" % r, tag="bank%d" % r)
-            product(res[:], halves[1], r)
-            copy(staged[:, r * HALF : (r + 1) * HALF], res[:])
-        nc.sync.dma_start(out_rows[:, :, halves[1]], staged[:].rearrange("p (r n) -> p r n", r=2))
+        for c, banks in enumerate((("bank6", "bank7"), ("bank4", "bank5"))):
+            staged = keep.tile([P, 2, CHUNK], F32, name="staged%d" % c)
+            by_parts(c, staged[:], banks)
+            nc.sync.dma_start(out_rows[:, :, c * CHUNK : (c + 1) * CHUNK], staged[:])
+
+        staged = keep.tile([P, 2, HALF], F32, name="staged_upper")
+        res = psum.tile([P, 2, CHUNK], F32, name="res2", tag="bank2")
+        for r in range(2):
+            product(res[:, r, :], slice(HALF, HALF + CHUNK), r)
+        on_vector(staged[:, :, :CHUNK], res[:])
+        by_parts(3, staged[:, :, CHUNK:], ("bank0", "bank1"))
+        nc.sync.dma_start(out_rows[:, :, halves[1]], staged[:])

@@ -18,7 +18,6 @@ ALU = mybir.AluOpType
 P = 128
 PACK = 4
 QUADRANT = 32
-QUADRANTS = P // QUADRANT
 SCALE_ROWS = 4
 GROUP = 16
 HALF = S // 2
@@ -44,11 +43,8 @@ def tile_picked_deepset_relu_p_kernel(tc, x_words, x_scales, w1, w2_words, w2_sc
         nc.vector.memset(w2s[:].bitcast(I32), 0)
 
         def load_scale_rows(tile, scales):
-            for q in range(QUADRANTS):
-                nc.sync.dma_start(
-                    tile[QUADRANT * q : QUADRANT * q + SCALE_ROWS, :].bitcast(I32),
-                    scales[0, SCALE_ROWS * q : SCALE_ROWS * (q + 1), :].bitcast(I32),
-                )
+            for r in range(SCALE_ROWS):
+                nc.sync.dma_start(tile[r:P:QUADRANT, :].bitcast(I32), scales[0, r :: SCALE_ROWS, :].bitcast(I32))
 
         w1_rows = w1.rearrange("(p j) c -> p (j c)", j=PACK)
         nc.sync.dma_start(early[:], w1_rows[:, :CUT])

@@ -52,7 +52,9 @@ def tile_picked_deepset_relu_p_kernel(tc, x_words, x_scales, w1, w2_words, w2_sc
         load_scale_rows(xs, x_scales)
         nc.sync.dma_start(xw[:].bitcast(I32), x_words[0].rearrange("p n t -> p (n t)").bitcast(I32))
         nc.sync.dma_start(late[:], w1_rows[:, CUT:])
-        load_scale_rows(w2s, w2_scales)
+        for first in range(2 * SCALE_ROWS):
+            row = QUADRANT * (first // SCALE_ROWS) + first % SCALE_ROWS
+            nc.sync.dma_start(w2s[row : P : P // 2, :].bitcast(I32), w2_scales[0, first :: 2 * SCALE_ROWS, :].bitcast(I32))
 
         xgs = keep.tile([P, S], U8, name="xgs", align_bytes=64)
         xg = keep.tile([P, S], U32, name="xg", align_bytes=64)
@@ -91,7 +93,9 @@ def tile_picked_deepset_relu_p_kernel(tc, x_words, x_scales, w1, w2_words, w2_sc
         cast(nc.scalar.copy, 0, 0, 2, 4)
         cast(nc.scalar.copy, 0, 1, 2, 4)
         w2w = keep.tile([P, N], U32, name="w2w", tag="early", align_bytes=64)
-        nc.sync.dma_start(w2w[:].bitcast(I32), w2_words[0].rearrange("p n t -> p (n t)").bitcast(I32))
+        w2_rows = w2_words[0].rearrange("p n t -> p (n t)").bitcast(I32)
+        for side in (slice(0, P // 2), slice(P // 2, P)):
+            nc.sync.dma_start(w2w[side, :].bitcast(I32), w2_rows[side, :])
 
         cast(nc.vector.tensor_copy, 1, 1, 0, 1)
         cast(nc.scalar.copy, 1, 0, 0, 1)
@@ -191,21 +195,14 @@ def tile_picked_deepset_relu_p_kernel(tc, x_words, x_scales, w1, w2_words, w2_sc
                 rhs=zq[:, members].bitcast(FP8X4), rhs_scale=zs[:, members], start=True, stop=True,
             )
 
-        def by_parts(c, dst, banks):
+        def by_parts(c, dst, banks, empty):
             for r in range(2):
                 res = psum.tile([P, CHUNK], F32, name="res%d_%d" % (c, r), tag=banks[r])
                 product(res[:], slice(c * CHUNK, (c + 1) * CHUNK), r)
-                on_scalar(dst[:, r, :], res[:])
+                empty(dst[:, r, :], res[:])
 
-        for c, banks in enumerate((("bank6", "bank7"), ("bank4", "bank5"))):
+        for c, banks in enumerate((("bank6", "bank7"), ("bank4", "bank5"), ("bank2", "bank3"), ("bank0", "bank1"))):
             staged = keep.tile([P, 2, CHUNK], F32, name="staged%d" % c)
-            by_parts(c, staged[:], banks)
-            nc.sync.dma_start(out_rows[:, :, c * CHUNK : (c + 1) * CHUNK], staged[:])
-
-        staged = keep.tile([P, 2, HALF], F32, name="staged_upper")
-        res = psum.tile([P, 2, CHUNK], F32, name="res2", tag="bank2")
-        for r in range(2):
-            product(res[:, r, :], slice(HALF, HALF + CHUNK), r)
-        on_vector(staged[:, :, :CHUNK], res[:])
-        by_parts(3, staged[:, :, CHUNK:], ("bank0", "bank1"))
-        nc.sync.dma_start(out_rows[:, :, halves[1]], staged[:])
+            by_parts(c, staged[:], banks, on_vector if c == 2 else on_scalar)
+            for parts in (slice(0, 1), slice(1, 2)) if c in (0, CHUNKS - 1) else (slice(0, 2),):
+                nc.sync.dma_start(out_rows[:, parts, c * CHUNK : (c + 1) * CHUNK], staged[:, parts, :])

from contextlib import ExitStack

import concourse.mybir as mybir

K, T, S, H, N = 512, 1024, 512, 512, 256
FLOPS = 2 * K * H * S + 2 * H * N * S

F32 = mybir.dt.float32
BF16 = mybir.dt.bfloat16
I32 = mybir.dt.int32
U32 = mybir.dt.uint32
U16 = mybir.dt.uint16
U8 = mybir.dt.uint8
FP8X4 = mybir.dt.float8_e4m3fn_x4
ACT = mybir.ActivationFunctionType
ALU = mybir.AluOpType

P = 128
PACK = 4
QUADRANT = 32
SCALE_ROWS = 4
GROUP = 16
HALF = S // 2
CHUNK = 128
CHUNKS = S // CHUNK
CUT = H + H // 2


def tile_picked_deepset_relu_p_kernel(tc, x_words, x_scales, w1, w2_words, w2_scales, offs, out):
    nc = tc.nc
    with ExitStack() as ctx:
        keep = ctx.enter_context(tc.tile_pool(name="keep", bufs=1))
        psum = ctx.enter_context(tc.psum_pool(name="psum", bufs=1))

        offsets = keep.tile([P, S // GROUP], U16, name="offsets")
        xw = keep.tile([P, T], U32, name="xw", align_bytes=64)
        xs = keep.tile([P, T], U8, name="xs", align_bytes=64)
        w2s = keep.tile([P, N], U8, name="w2s", align_bytes=64)
        early = keep.tile([P, CUT], F32, name="early", tag="early", align_bytes=64)
        late = keep.tile([P, PACK * H - CUT], F32, name="late", align_bytes=64)

        nc.vector.memset(xs[:].bitcast(I32), 0)
        nc.vector.memset(w2s[:].bitcast(I32), 0)

        def load_scale_rows(tile, scales):
            for r in range(SCALE_ROWS):
                nc.sync.dma_start(tile[r:P:QUADRANT, :].bitcast(I32), scales[0, r :: SCALE_ROWS, :].bitcast(I32))

        w1_rows = w1.rearrange("(p j) c -> p (j c)", j=PACK)
        nc.sync.dma_start(early[:], w1_rows[:, :CUT])
        nc.sync.dma_start(offsets[:], offs)
        load_scale_rows(xs, x_scales)
        nc.sync.dma_start(xw[:].bitcast(I32), x_words[0].rearrange("p n t -> p (n t)").bitcast(I32))
        nc.sync.dma_start(late[:], w1_rows[:, CUT:])
        for first in range(2 * SCALE_ROWS):
            row = QUADRANT * (first // SCALE_ROWS) + first % SCALE_ROWS
            nc.sync.dma_start(w2s[row : P : P // 2, :].bitcast(I32), w2_scales[0, first :: 2 * SCALE_ROWS, :].bitcast(I32))

        xgs = keep.tile([P, S], U8, name="xgs", align_bytes=64)
        xg = keep.tile([P, S], U32, name="xg", align_bytes=64)
        nc.vector.tensor_copy(xgs[:], xs[:].indirect(offsets[:]))
        for members in (slice(0, CHUNK), slice(CHUNK, S)):
            entries = offsets[:, members.start // GROUP : members.stop // GROUP]
            nc.vector.tensor_copy(xg[:, members], xw[:].indirect(entries))

        def warm_up(dst, members):
            nc.tensor.matmul_mx(
                out=dst, lhsT=xg[:, :QUADRANT].bitcast(FP8X4), lhsT_scale=xgs[:, :QUADRANT],
                rhs=xg[:, members].bitcast(FP8X4), rhs_scale=xgs[:, members], start=True, stop=True,
            )

        idle = [psum.tile([QUADRANT, S], F32, name="idle%d" % b, tag="bank%d" % b) for b in (6, 7)]
        for c in range(CHUNKS):
            warm_up(idle[0][:, c * CHUNK : (c + 1) * CHUNK], slice(0, CHUNK))
        warm_up(idle[1][:], slice(0, S))

        grouped = [keep.tile([P, 2, P, PACK], BF16, name="grouped%d" % v, align_bytes=64) for v in range(2)]
        wq = [keep.tile([P, P], U32, name="wq%d" % t, align_bytes=64) for t in range(PACK)]
        ws = [keep.tile([P, P], U8, name="ws%d" % t, align_bytes=64) for t in range(PACK)]

        def cast(copy, piece, side, t0, t1):
            split = 2 - side
            j0, j1 = (0, split) if piece == 0 else (split, PACK)
            source, start = (early, 0) if piece == 0 else (late, CUT)
            first = 2 * j0 + side - start // (H // 2)
            half_rows = source[:].rearrange("p (r m t) -> p m r t", m=P // 2, t=PACK)
            columns = slice(side * (P // 2), (side + 1) * (P // 2))
            dst = grouped[t0 // 2][:, t0 % 2 : t0 % 2 + t1 - t0, columns, j0:j1].rearrange("p t m j -> p m j t")
            copy(dst, half_rows[:, :, first : first + 2 * (j1 - j0) - 1 : 2, t0:t1])

        cast(nc.vector.tensor_copy, 0, 1, 0, 2)
        cast(nc.scalar.copy, 0, 0, 0, 2)
        cast(nc.scalar.copy, 0, 0, 2, 4)
        cast(nc.scalar.copy, 0, 1, 2, 4)
        w2w = keep.tile([P, N], U32, name="w2w", tag="early", align_bytes=64)
        w2_rows = w2_words[0].rearrange("p n t -> p (n t)").bitcast(I32)
        for side in (slice(0, P // 2), slice(P // 2, P)):
            nc.sync.dma_start(w2w[side, :].bitcast(I32), w2_rows[side, :])

        cast(nc.vector.tensor_copy, 1, 1, 0, 1)
        cast(nc.scalar.copy, 1, 0, 0, 1)
        cast(nc.vector.tensor_copy, 1, 1, 1, 2)
        cast(nc.vector.tensor_copy, 1, 0, 1, 2)
        cast(nc.scalar.copy, 1, 0, 2, 4)
        cast(nc.scalar.copy, 1, 1, 2, 4)
        for t in range(PACK):
            nc.vector.quantize_mx(
                out=wq[t][:].bitcast(FP8X4),
                scales=ws[t][:],
                in_=grouped[t // 2][:, t % 2, :, :].rearrange("p m j -> p (m j)"),
            )

        halves = [slice(a * HALF, (a + 1) * HALF) for a in range(2)]
        h = [keep.tile([P, S], F32, name="h%d" % t, align_bytes=64) for t in range(PACK)]
        total = [keep.tile([P, 1], F32, name="total%d" % t) for t in range(PACK)]
        pairs = [keep.tile([P, 2, 2, CHUNK, 2], BF16, name="pairs%d" % a, align_bytes=64) for a in range(2)]
        zi = [keep.tile([P, PACK * CHUNK], BF16, name="zi%d" % c, align_bytes=64) for c in range(CHUNKS)]

        def first_layer(t, spans, bank):
            first = spans[0].start
            acc = psum.tile([P, spans[-1].stop - first], F32, name="acc_" + bank, tag=bank)
            for members in spans:
                nc.tensor.matmul_mx(
                    out=acc[:, members.start - first : members.stop - first],
                    lhsT=wq[t][:].bitcast(FP8X4), lhsT_scale=ws[t][:],
                    rhs=xg[:, members].bitcast(FP8X4), rhs_scale=xgs[:, members], start=True, stop=True,
                )
            return acc

        head = keep.tile([P, 1], F32, name="head")
        acc = first_layer(0, [slice(0, CHUNK)], "bank4")
        nc.scalar.activation(h[0][:, :CHUNK], acc[:], ACT.Relu, accum_out=head[:])
        acc = first_layer(1, [slice(0, S)], "bank1")
        nc.scalar.activation(h[1][:], acc[:], ACT.Relu, accum_out=total[1][:])
        acc = first_layer(0, [slice(CHUNK, HALF), halves[1]], "bank0")
        nc.vector.tensor_scalar(
            out=h[0][:, CHUNK:], in0=acc[:], scalar1=0.0, scalar2=head[:],
            op0=ALU.max, op1=ALU.add, accum_out=total[0][:],
        )
        for t in range(2, PACK):
            acc = first_layer(t, [slice(0, S)], "bank%d" % t)
            nc.scalar.activation(h[t][:], acc[:], ACT.Relu, accum_out=total[t][:])

        def chunks_of(t, c0, c1):
            src = h[t][:, c0 * CHUNK : c1 * CHUNK].rearrange("p (b n) -> p b n", n=CHUNK)
            return pairs[c0 // 2][:, c0 % 2 : c0 % 2 + c1 - c0, t // 2, :, t % 2], src

        def centre(t, c0, c1):
            dst, src = chunks_of(t, c0, c1)
            nc.vector.tensor_scalar(
                out=dst, in0=src, scalar1=-float(S), scalar2=total[t][:], op0=ALU.mult, op1=ALU.add
            )

        def centre_on_scalar(t, c):
            dst, src = chunks_of(t, c, c + 1)
            nc.scalar.activation(dst, src, ACT.Identity, scale=-float(S), bias=total[t][:])

        for t in (1, 0):
            for a in range(2):
                centre(t, 2 * a, 2 * a + 2)
        for t in range(2, PACK):
            centre(t, 0, 2)
        for t in range(2, PACK):
            centre(t, 2, 3)
            centre_on_scalar(t, 3)

        zq = keep.tile([P, S], U32, name="zq", align_bytes=64)
        zs = keep.tile([P, S], U8, name="zs", align_bytes=64)

        def weave(copy, c):
            words = pairs[c // 2][:, c % 2, :, :, :].rearrange("p v n e -> p v (n e)").bitcast(F32)
            copy(zi[c][:].bitcast(F32).rearrange("p (n v) -> p n v", v=2), words.rearrange("p v n -> p n v"))

        def quantize_z(c):
            members = slice(c * CHUNK, (c + 1) * CHUNK)
            nc.vector.quantize_mx(out=zq[:, members].bitcast(FP8X4), scales=zs[:, members], in_=zi[c][:])

        for c in range(CHUNKS):
            weave(nc.scalar.copy if c % 2 else nc.vector.tensor_copy, c)
        for c in range(CHUNKS):
            quantize_z(c)

        out_rows = out.rearrange("(r p) n -> p r n", p=P)

        def on_scalar(dst, src):
            nc.scalar.activation(dst, src, ACT.Copy, scale=-1.0 / S)

        def on_vector(dst, src):
            nc.vector.tensor_scalar(out=dst, in0=src, scalar1=-1.0 / S, scalar2=None, op0=ALU.mult)

        def product(dst, members, r):
            rows = slice(r * P, (r + 1) * P)
            nc.tensor.matmul_mx(
                out=dst, lhsT=w2w[:, rows].bitcast(FP8X4), lhsT_scale=w2s[:, rows],
                rhs=zq[:, members].bitcast(FP8X4), rhs_scale=zs[:, members], start=True, stop=True,
            )

        def by_parts(c, dst, banks, empty):
            for r in range(2):
                res = psum.tile([P, CHUNK], F32, name="res%d_%d" % (c, r), tag=banks[r])
                product(res[:], slice(c * CHUNK, (c + 1) * CHUNK), r)
                empty(dst[:, r, :], res[:])

        for c, banks in enumerate((("bank6", "bank7"), ("bank4", "bank5"), ("bank2", "bank3"), ("bank0", "bank1"))):
            staged = keep.tile([P, 2, CHUNK], F32, name="staged%d" % c)
            by_parts(c, staged[:], banks, on_vector if c == 2 else on_scalar)
            for parts in (slice(0, 1), slice(1, 2)) if c in (0, CHUNKS - 1) else (slice(0, 2),):
                nc.sync.dma_start(out_rows[:, parts, c * CHUNK : (c + 1) * CHUNK], staged[:, parts, :])
